import numpy as np, ml_dtypes
CORES = [40,64,80,88,96,104,120,144]
N = 8
import mx_ref
BF = ml_dtypes.bfloat16
def f(rng, *shape):
    return mx_ref.flush((rng.standard_normal(shape, dtype=np.float32) * np.exp2(rng.integers(-2, 3, shape[:-1] + (1,)))).astype(BF))
def wide(rng, *shape, cols=0):
    v = rng.standard_normal(shape, dtype=np.float32) * np.exp2(rng.integers(-12, 13, shape)).astype(np.float32)
    if cols: v *= np.repeat(np.exp2(rng.integers(-cols, cols + 1, shape[:-2] + (1, shape[-1] // 4))) * (rng.random(shape[:-2] + (1, shape[-1] // 4)) > 0.0625), 4, axis=-1).astype(np.float32)
    return mx_ref.flush(v.astype(BF))
T, CAPP, O = 256, 64, 1
def scores(us, x):
    return mx_ref.matmul(mx_ref.quantize(us), mx_ref.quantize(x))[:8] + np.float32(0.0)
def winners(us, x):
    return np.argmax(np.stack([scores(us[s], x[s]) for s in range(N)]), axis=0)
def fill(rng, n, tot, most):
    n = np.array(n)
    while n.sum() < tot:
        q = rng.integers(0, N)
        if n[q] < most[q]: n[q] += 1
    return rng.permutation(np.repeat(np.arange(N), n))
def deal(rng, full):
    return np.stack([fill(rng, [CAPP if q in full[g] else 0 for q in range(N)], T, [CAPP] * N) for g in range(8)])
def one(rng):
    g, s = rng.integers(0, 8), rng.integers(0, N)
    return deal(rng, [[s] if i == g else [] for i in range(8)])
def heads(rng):
    u, h = np.zeros((8, 16, 128, 4), np.float32), np.arange(8)
    u[h, :, h] = rng.choice([-1.0, 1.0], (8, 16, 4)) * (0.25 + np.abs(rng.standard_normal((8, 16, 4)))) * np.exp2(rng.integers(-2, 3, (8, 16, 1)))
    return np.repeat(u.reshape(1, 128, 512).astype(BF), N, axis=0)
def plant(rng, x, us, wn, big=4, tie=None, zero=None):
    v = np.abs(x.astype(np.float32)).reshape(N, 8, 16, T, 4)
    v[v < 2.0 ** -24] = 0
    h, b = np.arange(8), np.float32(big)
    a = np.sign(us.astype(np.float32)).reshape(8, 16, 128, 4)[h, :, h][:, :, None]
    win = (wn == np.arange(N)[:, None, None])[:, :, None, :, None]
    neg = (rng.random((8, T)) < 0.125)[:, None, :, None]
    c = np.where(rng.random(v.shape, dtype=np.float32) < 0.5, np.float32(-1), np.float32(1))
    t = (np.where(neg, np.where(win, -a, -4 * b * a), np.where(win, b * a, c)) * v).astype(np.float32)
    s = np.stack([scores(us, t[r].reshape(128, 4 * T).astype(BF)) for r in range(N)])
    won = np.take_along_axis(s, wn[None], axis=0)[0]
    lost = np.where(win[:, :, 0, :, 0], -np.inf, s).max(axis=0)
    bad = (~(won - lost > 0.5 * np.abs(won)))[:, None, :, None]
    t = np.where(bad, np.where(win, b * a, -a) * v, t).astype(np.float32)
    if tie is not None:
        best = np.where(win, t, np.float32(0)).sum(axis=0)
        t = np.where(tie[:, None, :, None] & (wn < np.arange(N)[:, None, None])[:, :, None, :, None], best, t)
    if zero is not None: t[:, :, :, zero] = 0
    return t.reshape(N, 128, 4 * T).astype(BF)
def narrow(rng, x, us, wn):
    v, h = x.astype(np.float32).reshape(N, 8, 16, T, 4), np.arange(8)
    u = np.abs(us.astype(np.float32)).reshape(8, 16, 128, 4)[h, :, h]
    i, b = np.unravel_index(u.reshape(8, 64).argmin(axis=1), (16, 4))
    win = wn == np.arange(N)[:, None, None]
    part = np.where(win[:, :, None, :, None], v, np.float32(0)).sum(axis=0)
    p = np.exp2(np.floor(np.log2((u[:, :, None] * np.abs(part)).sum(axis=(1, 3))) - np.log2(u[h, i, b])[:, None]) - 12)
    z = np.stack([np.where(part[g, i[g], :, b[g]] < 0, -p[g], p[g]) for g in range(8)])
    close = np.repeat((rng.permutation(T) < T // 3)[None], 8, axis=0)
    other = (wn + rng.integers(1, N, (8, T))) % N
    hold = ((rng.random((N, 8, T)) < 0.25) | (other == np.arange(N)[:, None, None])) & ~win & close
    held = hold | (win & close)
    t = np.where(held[:, :, None, :, None], part, v).astype(np.float32)
    d = np.where(hold, rng.choice([-0.125, 0.125], (N, 8, T)), 0.0)
    for k in range(2):
        for g in range(8): t[:, g, i[g], :, b[g]] = np.where(held[:, g], z[g] * (1.5 + d[:, g]), t[:, g, i[g], :, b[g]])
        s = np.stack([scores(us, t[r].reshape(128, 4 * T).astype(BF)) for r in range(N)])
        if k == 0: d = np.where(s == np.take_along_axis(s, wn[None], axis=0), 2 * d, d)
    now = np.argmax(s, axis=0)
    for g in range(8):
        for k in range(T):
            n = np.bincount(now[g], minlength=N)
            q = n.argmax()
            if n[q] <= CAPP: break
            j = rng.permutation(np.flatnonzero((now[g] == q) & (wn[g] != q)))[:n[q] - CAPP]
            now[g, j] = wn[g, j]; close[g, j] = False
    return np.where(close[:, None, :, None], t, v).reshape(N, 128, 4 * T).astype(BF)
def draw(rng, wn, **k):
    us = heads(rng)
    return {"x": plant(rng, f(rng, N, 128, 4 * T), us[0], wn, **k), "us": us, "w": f(rng, N, 128, 512 * O)}
def setup_inputs(rng):
    return draw(rng, one(rng))
def setup_inputs_equal(rng):
    e, p = CAPP - 8, rng.permutation(T)
    far = np.stack([fill(rng, [8] + [0] * (N - 1), T - e, [8] + [CAPP] * (N - 1)) for g in range(8)])
    wn = np.concatenate([np.zeros((8, e), int), far], axis=1)[:, p]
    tie = np.repeat(np.concatenate([np.ones(e, bool), np.arange(T - e) % 2 == 0])[None], 8, axis=0)[:, p]
    return draw(rng, wn, tie=tie, zero=(np.arange(T) < 4)[p])
def setup_inputs_full(rng):
    s, k = int(rng.integers(0, N)), T // CAPP
    return draw(rng, deal(rng, [[s] + [q for q in rng.permutation(N).tolist() if q != s][:k - 1] for g in range(8)]))
def setup_inputs_near(rng):
    wn = one(rng)
    d = draw(rng, wn); d["x"] = narrow(rng, d["x"], d["us"][0], wn); return d
def setup_inputs_spread(rng):
    wn, us = one(rng), heads(rng)
    e = np.exp2(rng.integers(-4, 5, (N, 8, 1, T, 1))) * ((rng.random((N, 8, 1, T, 1)) > 0.0625) | (wn == np.arange(N)[:, None, None])[:, :, None, :, None])
    x = wide(rng, N, 128, 4 * T).astype(np.float32).reshape(N, 8, 16, T, 4) * e.astype(np.float32)
    return {"x": plant(rng, x, us[0], wn, big=256), "us": us, "w": f(rng, N, 128, 512 * O)}
def setup_inputs_stretch(rng):
    L = []
    for g in range(8):
        s, a = rng.integers(0, N), rng.choice([0, T - CAPP, rng.integers(0, T - CAPP + 1)])
        far = fill(rng, [0] * N, T - CAPP, [0 if q == s else CAPP for q in range(N)])
        L.append(np.concatenate([far[:a], np.full(CAPP, s), far[a:]]))
    return draw(rng, np.stack(L))
def check_inputs(d):
    b = []
    for k in ("x", "us", "w"):
        v = np.abs(np.asarray(d[k]).astype(np.float32))
        if not ((v == 0) | ((v >= 2.0 ** -30) & (v <= 2.0 ** 30))).all(): b.append(k)
    if b: return b
    u, h = np.array(d["us"]).astype(np.float32), np.arange(8)
    same = (u == u[:1]).all()
    u = u.reshape(N, 8, 16, 128, 4); u[:, h, :, h] = 0
    if not same or (u != 0).any(): b.append("us")
    wn = winners(d["us"], d["x"])
    if max((wn == s).sum(axis=1).max() for s in range(N)) > CAPP: b.append("x")
    return b
def reference(x, us, w):
    wn = winners(us, x)
    M = []
    for s in range(N):
        v = np.where((wn == s)[:, None, :, None], x[s].astype(np.float32).reshape(8, 16, T, 4), np.float32(0))
        M.append(mx_ref.quantize(np.ascontiguousarray(v.reshape(128, 4 * T).astype(BF))))
    y = np.zeros((N, 128, O * T), np.float32)
    for r in range(N):
        for o in range(O):
            W = mx_ref.quantize(np.ascontiguousarray(w[r][:, 512 * o:512 * o + 512]))
            for s in range(N): y[r][:, T * o:T * o + T] += mx_ref.matmul(W, M[s])
    return {"y": y, "wn": np.repeat(wn.astype(np.float32)[None], N, axis=0)}

@@ -1,0 +1,340 @@
+from concourse.bass import DstId, RemoteDMATransfer
+from concourse.mybir import dt, AluOpType as A, ActivationFunctionType
+
+N = 8
+CODES = "float8_e4m3fn_x4"
+ROW = 80
+WIN = 17 * ROW
+SCRATCH = {
+    "xb": ("sbuf", [128, 1024], "bfloat16"),
+    "usl": ("sbuf", [128, 32], "bfloat16"),
+    "zb": ("sbuf", [128, 560], "bfloat16"),
+    "pk": ("sbuf", [128, 512], "bfloat16"),
+    "wz": ("sbuf", [128, 4096], "bfloat16"),
+    "zq": ("sbuf", [128, 140], CODES), "zp": ("sbuf", [128, 140], "uint8"),
+    "xq": ("sbuf", [128, 384], CODES), "xp": ("sbuf", [128, 384], "uint8"),
+    "wq": ("sbuf", [128, 1024], CODES), "wp": ("sbuf", [128, 1024], "uint8"),
+    "oq": ("sbuf", [128, 128], CODES), "op": ("sbuf", [128, 128], "uint8"),
+    "pq": ("sbuf", [128, 512], CODES), "pp": ("sbuf", [128, 512], "uint8"),
+    "rq": ("sbuf", [128, 64], CODES), "rp": ("sbuf", [128, 64], "uint8"),
+    "rsc": ("sbuf", [128, 16], "float32"),
+    "pi": ("sbuf", [128, 1], "int32"), "pj": ("sbuf", [128, 4], "int32"), "pf": ("sbuf", [128, 4], "float32"),
+    "c64": ("sbuf", [128, 64], "float32"), "d64": ("sbuf", [128, 64], "float32"), "m4": ("sbuf", [128, 64], "float32"),
+    "msk": ("sbuf", [128, 64], "float32"), "mk2": ("sbuf", [128, 64], "float32"),
+    "v0": ("sbuf", [128, 256], "float32"), "val": ("sbuf", [128, 256], "float32"),
+    "pc0": ("sbuf", [128, 16], "float32"), "pc": ("sbuf", [128, 16], "float32"), "qr": ("sbuf", [128, 1], "float32"),
+    "one": ("sbuf", [128, 16], "float32"), "rm": ("sbuf", [128, 128], "float32"), "nr": ("sbuf", [128, 128], "float32"),
+    "k0": ("sbuf", [128, 128], "float32"), "k1": ("sbuf", [128, 128], "float32"), "prio": ("sbuf", [128, 128], "float32"),
+    "sm": ("sbuf", [128, 64], "float32"), "s32": ("sbuf", [128, 32], "float32"),
+    "sc": ("sbuf", [128, 128], "float32"), "repa": ("sbuf", [128, 64], "float32"), "repb": ("sbuf", [128, 64], "float32"),
+    "la": ("sbuf", [128, 64], "float32"), "la2": ("sbuf", [128, 32], "float32"), "la3": ("sbuf", [128, 16], "float32"),
+    "pen": ("sbuf", [128, 16], "float32"),
+    "cb": ("sbuf", [128, 64], "float32"), "cb2": ("sbuf", [128, 32], "float32"), "lose": ("sbuf", [128, 16], "float32"),
+    "tb": ("sbuf", [128, 32], "float32"), "tt": ("sbuf", [128, 32], "float32"), "ts": ("sbuf", [128, 32], "float32"),
+    "bt": ("sbuf", [128, 32], "float32"), "lp": ("sbuf", [128, 16], "float32"), "fo": ("sbuf", [128, 16], "float32"),
+    "offa": ("sbuf", [128, 16], "uint16"), "offb": ("sbuf", [128, 16], "uint16"),
+    "inv": ("sbuf", [128, WIN], "float32"), "mkd": ("sbuf", [128, 64], "float32"), "sel": ("sbuf", [128, 64], "float32"),
+    "m64": ("sbuf", [128, 64], "float32"), "m32": ("sbuf", [128, 32], "float32"), "m16": ("sbuf", [128, 16], "float32"),
+    "eq": ("sbuf", [128, 128], "float32"), "eqp": ("sbuf", [128, 128], "float32"),
+    "e64": ("sbuf", [128, 64], "float32"), "e32": ("sbuf", [128, 32], "float32"), "pv": ("sbuf", [128, 16], "float32"),
+    "wnv": ("sbuf", [128, 16], "float32"), "win": ("sbuf", [128, 128], "float32"), "win2": ("sbuf", [128, 128], "float32"),
+    "cum": ("sbuf", [128, 128], "float32"), "t2": ("sbuf", [128, 128], "float32"), "ts2": ("sbuf", [128, 128], "float32"),
+    "b2": ("sbuf", [128, 128], "float32"), "cu2": ("sbuf", [128, 128], "float32"), "pr": ("sbuf", [128, 128], "float32"),
+    "f64": ("sbuf", [128, 64], "float32"), "f32": ("sbuf", [128, 32], "float32"), "x1": ("sbuf", [128, 32], "float32"),
+    "t1": ("sbuf", [128, 32], "float32"), "off": ("sbuf", [128, 128], "uint16"),
+    "ps": ("psum", [128, 4096], "float32"),
+    "res": ("sbuf", [128, 4096], "float32"),
+    "ya": ("sbuf", [128, 256], "float32"), "yb": ("sbuf", [128, 256], "float32"),
+}
+SEMAPHORES = (["cv", "loc", "scA", "scB", "cqA", "cqB", "rs0", "rs1", "rs2",
+               "lus", "lx", "lw0", "lw1", "lown", "lwn", "ly",
+               "kz", "kzs", "kzq", "kxp", "kxq", "ksc", "ksr", "kps", "kpsr", "kio", "kw0", "kw1", "kwq0", "kwq1", "kpk", "kwn", "ky"]
+              + ["%s%d" % (k, h) for k in ("ma", "da", "mb", "db") for h in range(8)])
+
+
+def roads(core, T, topo):
+    others = [c for c in T.cores if c != core]
+    near = [c for c in others if topo.may_write(core, c)]
+    far = [c for c in others if not topo.may_write(core, c)]
+    help_ = [c for c in topo.cores_of(core) if c not in T.cores and all(topo.may_write(c, d) for d in far)]
+    help_.sort(key=lambda c: topo.die(c) == topo.die(core))
+    help_ = help_[:2]
+    share = {h: far[k::len(help_)] for k, h in enumerate(help_)}
+    return near, far, help_, share
+
+
+def order(T, topo):
+    a = [c for c in T.cores if c == T.cores[0] or topo.may_write(T.cores[0], c)]
+    return [a, [c for c in T.cores if c not in a]]
+
+
+def bits(engines):
+    return sum(1 << e for e in engines)
+
+
+def ids(core, dests, topo):
+    r = []
+    for d in dests:
+        rid, pid = topo.addr(d, core)
+        r.append(DstId(rid=rid, pnc=pid))
+    return r
+
+
+def relay(g, core, boss, dests, T, topo):
+    p = sum(order(T, topo), []).index(boss)
+    eng = topo.engines(core, dests[0])
+
+    def send(src, dst, sem):
+        g.remote_dma_fused([RemoteDMATransfer(dst_ids=ids(core, dests, topo), dma_engine_mask=bits(eng), remote_sem=sem,
+                                              srcs=[src], dsts=[dst] * len(dests))], local_sem=T.sem.loc)
+    k = len([e for e in topo.engines(boss, core) if e not in eng])
+    g.wait_ge(T.sem.rs0, k)
+    send(T.rsc[:], T.sc[:, 16 * p:16 * p + 16], T.sem.scB)
+    g.wait_ge(T.sem.rs1, k)
+    send(T.rq[:].bitcast(dt.uint8), T.pq[:, 64 * p:64 * p + 64].bitcast(dt.uint8), T.sem.cqB)
+    g.wait_ge(T.sem.rs2, k)
+    send(T.rp[:], T.pp[:, 64 * p:64 * p + 64], T.sem.cqB)
+    g.wait_ge(T.sem.loc, 3 * len(eng))
+
+
+def rank_program(g, core, T, topo):
+    rank = T.rank_of(core)
+    if rank is None:
+        for boss in T.cores:
+            if core in topo.cores_of(boss):
+                share = roads(boss, T, topo)[3]
+                if core in share:
+                    relay(g, core, boss, share[core], T, topo)
+        return
+    near, far, helpers, share = roads(core, T, topo)
+    planes = order(T, topo)
+    pieces = planes[0] + planes[1]
+    cls = 0 if core in planes[0] else 1
+    mine = pieces.index(core)
+    idx = planes[cls].index(core)
+    rk = [T.rank_of(c) for c in pieces]
+
+    Q = {"v": [g.vector, "cv"], "s": [g.scalar, None], "t": [g.tensor, None], "g": [g, None], "y": [g.sync, None]}
+    total = {}
+    seen = {q: {} for q in Q}
+
+    def wait(q, *deps):
+        for d in deps:
+            if d is None:
+                continue
+            sem, val = d
+            if sem == Q[q][1]:
+                val = total[sem]
+            if seen[q].get(sem, 0) < val:
+                Q[q][0].wait_ge(T.sem[sem], val)
+                seen[q][sem] = val
+
+    def run(q, ins, key=None, n=1):
+        sem = key or Q[q][1]
+        ins.then_inc(T.sem[sem], n)
+        total[sem] = total.get(sem, 0) + n
+        return (sem, total[sem])
+
+    def V(name, *args, deps=(), key=None):
+        wait("v", *deps)
+        f = {"set": g.vector.memset, "cp": g.vector.tensor_copy, "tt": g.vector.tensor_tensor, "ts": g.vector.tensor_scalar,
+             "scan": g.vector.tensor_tensor_scan, "tr": g.vector.transpose, "q": g.vector.quantize_mx}[name]
+        return run("v", f(*args), key)
+
+    def S(out, in_, deps=(), key=None):
+        wait("s", *deps)
+        return run("s", g.scalar.activation(out, in_, ActivationFunctionType.Copy), key)
+
+    def iota(out, pattern, base, cm):
+        return run("g", g.iota(out, pattern, base, cm, allow_small_or_imprecise_dtypes=True), "kio")
+
+    lus = run("y", g.sync.dma_start(T.usl[:], T.us[:, 0:32]), "lus", 16)
+    lx = run("s", g.scalar.dma_start(T.xb[:], T.x[:]), "lx", 16)
+
+    iota(T.pi[:], [[0, 1]], 0, 1)
+    iota(T.c64[:], [[1, 4], [0, 16]], 0, 0)
+    iota(T.d64[:], [[0, 16], [1, 4]], 0, 0)
+    iota(T.pc0[:], [[1, 16]], 0, 0)
+    iota(T.k0[:], [[64, 8], [0, 16]], -1, 0)
+    kio = iota(T.v0[:], [[4, 16], [64, 16]], 0, 0)
+
+    kz = V("set", T.zb[:], 0.0, key="kz")
+    zpk = V("set", T.pk[:], 0.0)
+    kxp = V("q", T.xq[:, 256:384], T.xp[:, 256:384], T.pk[:], deps=[zpk], key="kxp")
+    wait("v", kio)
+    V("ts", T.pj[:, 0:1], T.pi[:], 3, None, A.bitwise_and)
+    V("ts", T.pj[:, 1:2], T.pi[:], 2, 3, A.arith_shift_right, A.bitwise_and)
+    t = V("ts", T.pj[:, 2:3], T.pi[:], 15, None, A.bitwise_and)
+    t = V("cp", T.pf[:, 0:3], T.pj[:, 0:3], deps=[t])
+    pt, pa, pqq = T.pf[:, 0:1], T.pf[:, 1:2], T.pf[:, 2:3]
+    V("ts", T.msk[:], T.c64[:], pt, None, A.is_equal, deps=[t])
+    zs = ksz = None
+    for l in range(4):
+        for e in range(4):
+            a = 4 * (12 + l) + e
+            o, i = T.zb[:, a:a + 449:64], T.usl[:, e:32:4]
+            if l < 2:
+                zs = V("cp", o, i, deps=[kz, lus])
+            else:
+                ksz = S(o, i, deps=[kz, lus], key="kzs")
+    kzq = V("q", T.zq[:], T.zp[:], T.zb[:], deps=[zs, ksz], key="kzq")
+    kw0 = V("set", T.wz[:, 0:2048], 0.0, key="kw0")
+    kxq = V("q", T.xq[:, 0:256], T.xp[:, 0:256], T.xb[:], deps=[lx], key="kxq")
+
+    wait("t", kzq, kxp, kxq)
+    for i in range(4):
+        m = g.tensor.matmul_mx(T.ps[:, 0:128], T.zq[:, 12 - 4 * i:140 - 4 * i], T.zp[:, 12 - 4 * i:140 - 4 * i],
+                               T.xq[:, 64 * i:64 * i + 128], T.xp[:, 64 * i:64 * i + 128], i == 0, i == 3)
+    kps = run("t", m, "kps")
+    kpsr = V("tt", T.sm[:], T.ps[:, 0:64], T.msk[:], A.mult, deps=[kps], key="kpsr")
+    t = V("tt", T.s32[:], T.sm[:, 0:32], T.sm[:, 32:64], A.add, deps=[kpsr])
+    own = T.sc[:, 16 * mine:16 * mine + 16]
+    ksc = V("tt", own, T.s32[:, 0:16], T.s32[:, 16:32], A.add, deps=[t], key="ksc")
+
+    eoff = topo.engines(core, near[0])
+    eon = [e for e in topo.engines(core, helpers[0]) if e not in eoff]
+
+    def send(src, dst, hop, sem, hsem):
+        g.remote_dma_fused([
+            RemoteDMATransfer(dst_ids=ids(core, helpers, topo), dma_engine_mask=bits(eon), remote_sem=T.sem[hsem],
+                              srcs=[src], dsts=[hop] * len(helpers)),
+            RemoteDMATransfer(dst_ids=ids(core, near, topo), dma_engine_mask=bits(eoff), remote_sem=T.sem[sem],
+                              srcs=[src], dsts=[dst] * len(near))], local_sem=T.sem.loc)
+        total["loc"] = total.get("loc", 0) + len(eon) + len(eoff)
+    wait("g", ksc)
+    send(own, own, T.rsc[:], "scA", "rs0")
+    nA = len(near) * len(eoff)
+    nB = sum(len(topo.engines(roads(c, T, topo)[2][0], core)) for c in far)
+
+    ksr = None
+    for i in range(4):
+        ksr = S(T.repa[:, 16 * i:16 * i + 16], own, deps=[ksc], key="ksr")
+    kw1 = V("set", T.wz[:, 2048:4096], 0.0, key="kw1")
+    for half, kw in ((0, kw0), (1, kw1)):
+        wait("y", kw)
+        for h in range(4 * half, 4 * half + 4):
+            run("y", g.sync.dma_start(T.wz[16 * h:16 * h + 16, 512 * h:512 * h + 512], T.w[16 * h:16 * h + 16, :]), "lw%d" % half, 16)
+    V("set", T.la[:, 16 * idx:16 * idx + 16], 0.0)
+    V("set", T.one[:], 1.0)
+    t = V("set", T.rm[:], 1.0)
+    V("set", T.tb[:], 0.0)
+    V("set", T.ts[:], 0.0)
+    V("set", T.ts2[:, 0:1], 0.0)
+    V("set", T.inv[:, 0:64], 0.0)
+    t2 = V("ts", T.qr[:], pqq, float(ROW), float(ROW + 1), A.mult, A.add)
+    V("ts", T.m4[:], T.d64[:], 1.0, None, A.min)
+    V("ts", T.mk2[:], T.d64[:], pa, None, A.is_equal)
+    V("ts", T.val[:], T.v0[:], pt, None, A.add)
+    V("set", T.rm[:, 0:128:16], 0.0, deps=[t])
+    V("ts", T.pc[:], T.pc0[:], T.qr[:], None, A.add, deps=[t2])
+
+    ca, cb = 64 * cls, 64 * (1 - cls)
+    wait("v", ksr, ("scA", nA), ksc)
+    a = 16 * idx
+    if idx > 0:
+        t = V("tt", T.la[:, 0:a], T.sc[:, ca:ca + a], T.repa[:, 0:a], A.is_ge)
+    if idx < 3:
+        t = V("tt", T.la[:, a + 16:64], T.sc[:, ca + a + 16:ca + 64], T.repa[:, a + 16:64], A.is_gt)
+    t = V("tt", T.la2[:], T.la[:, 0:32], T.la[:, 32:64], A.max, deps=[t])
+    t = V("tt", T.la3[:], T.la2[:, 0:16], T.la2[:, 16:32], A.max, deps=[t])
+    t = V("ts", T.pen[:], T.la3[:], -1e28, None, A.mult, deps=[t])
+    for i in range(4):
+        tr = V("tt", T.repb[:, 16 * i:16 * i + 16], own, T.pen[:], A.add, deps=[t] if i == 0 else [])
+    for half in range(2):
+        wait("v", ("lw%d" % half, 64))
+        V("q", T.wq[:, 512 * half:512 * half + 512], T.wp[:, 512 * half:512 * half + 512],
+          T.wz[:, 2048 * half:2048 * half + 2048], key="kwq%d" % half)
+
+    wait("v", tr, ("scB", nB))
+    low = 16 * len([c for c in planes[1 - cls] if T.rank_of(c) < rank])
+    if low > 0:
+        t = V("tt", T.cb[:, 0:low], T.sc[:, cb:cb + low], T.repb[:, 0:low], A.is_ge)
+    if low < 64:
+        t = V("tt", T.cb[:, low:64], T.sc[:, cb + low:cb + 64], T.repb[:, low:64], A.is_gt)
+    t = V("tt", T.cb2[:], T.cb[:, 0:32], T.cb[:, 32:64], A.max, deps=[t])
+    t = V("tt", T.lose[:], T.cb2[:, 0:16], T.cb2[:, 16:32], A.max, deps=[t])
+    t = V("scan", T.tb[:, 0:16], T.one[:], T.lose[:], -1.0, A.add, A.subtract, deps=[t])
+    V("tt", T.lp[:], T.lose[:], T.pc[:], A.mult)
+    t = V("tr", T.tt[:], T.tb[:], deps=[t])
+    V("tt", T.fo[:], T.tb[:, 0:16], T.lp[:], A.add)
+    t = V("scan", T.ts[:, 1:32], T.tt[:, 0:31], T.rm[:, 1:32], 0.0, A.add, A.mult, deps=[t])
+    t = V("tr", T.bt[:], T.ts[:], deps=[t])
+    t = V("ts", T.offa[:], T.fo[:], T.bt[:, 15:16], pqq, A.add, A.add, deps=[t])
+    t = V("cp", T.inv[:, 0:WIN].indirect(T.offa[:, 0:16]), T.val[:], deps=[t])
+    t = V("tt", T.mkd[:], T.inv[:, 0:64], T.mk2[:], A.mult, deps=[t])
+    t = V("scan", T.sel[:], T.m4[:], T.mkd[:], 0.0, A.mult, A.add, deps=[t])
+    t = V("cp", T.offb[:], T.sel[:, 3:64:4], deps=[t])
+    t = V("cp", T.pk[:, 0:256], T.xb[:, 0:1024].indirect(T.offb[:, 0:16]), deps=[t])
+    kpk = V("q", T.oq[:], T.op[:], T.pk[:], deps=[t], key="kpk")
+
+    wait("g", kpk)
+    c0 = 64 * mine
+    send(T.oq[:, 0:64].bitcast(dt.uint8), T.pq[:, c0:c0 + 64].bitcast(dt.uint8), T.rq[:].bitcast(dt.uint8), "cqA", "rs1")
+    send(T.op[:, 0:64], T.pp[:, c0:c0 + 64], T.rp[:], "cqA", "rs2")
+    wait("y", kpk)
+    run("y", g.sync.dma_start(T.pq[:, c0:c0 + 64].bitcast(dt.uint8), T.oq[:, 0:64].bitcast(dt.uint8)), "lown", 16)
+    run("y", g.sync.dma_start(T.pp[:, c0:c0 + 64], T.op[:, 0:64]), "lown", 16)
+
+    t = V("tt", T.m64[:], T.sc[:, 0:64], T.sc[:, 64:128], A.max)
+    t = V("tt", T.m32[:], T.m64[:, 0:32], T.m64[:, 32:64], A.max, deps=[t])
+    t = V("tt", T.m16[:], T.m32[:, 0:16], T.m32[:, 16:32], A.max, deps=[t])
+    for i in range(8):
+        V("set", T.prio[:, 16 * i:16 * i + 16], float(8 - rk[i]))
+    for i in range(8):
+        t = V("tt", T.eq[:, 16 * i:16 * i + 16], T.sc[:, 16 * i:16 * i + 16], T.m16[:], A.is_equal, deps=[t] if i == 0 else [])
+    t = V("tt", T.eqp[:], T.eq[:], T.prio[:], A.mult, deps=[t])
+    t = V("tt", T.e64[:], T.eqp[:, 0:64], T.eqp[:, 64:128], A.max, deps=[t])
+    t = V("tt", T.e32[:], T.e64[:, 0:32], T.e64[:, 32:64], A.max, deps=[t])
+    t = V("tt", T.pv[:], T.e32[:, 0:16], T.e32[:, 16:32], A.max, deps=[t])
+    for i in range(8):
+        t = V("ts", T.win[:, 16 * i:16 * i + 16], T.pv[:], float(8 - rk[i]), None, A.is_equal, deps=[t] if i == 0 else [])
+    t = V("scan", T.cum[:], T.rm[:], T.win[:], 0.0, A.mult, A.add, deps=[t])
+    V("ts", T.nr[:], T.rm[:], -1.0, 1.0, A.mult, A.add)
+    kwn = V("ts", T.wnv[:], T.pv[:], -1.0, 8.0, A.mult, A.add, key="kwn")
+    t = V("tr", T.t2[:], T.cum[:], deps=[t])
+    V("tt", T.k1[:], T.k0[:], T.nr[:], A.mult)
+    t = V("scan", T.ts2[:, 1:128], T.t2[:, 0:127], T.rm[:, 1:128], 0.0, A.add, A.mult, deps=[t])
+    V("tt", T.win2[:], T.win[:], T.k1[:], A.add)
+    t = V("tr", T.b2[:], T.ts2[:], deps=[t])
+    t = V("tt", T.win2[:, 0:128:16], T.win2[:, 0:128:16], T.b2[:, 15:128:16], A.add, deps=[t])
+    t = V("scan", T.cu2[:], T.rm[:], T.win2[:], 0.0, A.mult, A.add, deps=[t])
+    t = V("tt", T.pr[:], T.cu2[:], T.win[:], A.mult, deps=[t])
+    t = V("tt", T.f64[:], T.pr[:, 0:64], T.pr[:, 64:128], A.add, deps=[t])
+    t = V("tt", T.f32[:], T.f64[:, 0:32], T.f64[:, 32:64], A.add, deps=[t])
+    V("tt", T.x1[:, 0:16], T.f32[:, 0:16], T.f32[:, 16:32], A.add, deps=[t])
+    t = V("tt", T.x1[:, 16:32], T.f32[:, 0:16], T.f32[:, 16:32], A.add)
+    t = V("tr", T.t1[:], T.x1[:], deps=[t])
+    for a in range(4):
+        for b in range(4):
+            t = V("cp", T.off[32 * b:32 * b + 32, 32 * a:32 * a + 32], T.t1[32 * a:32 * a + 32, 0:32], deps=[t] if a + b == 0 else [])
+    toff = t
+    wait("y", kwn)
+    run("y", g.sync.dma_start(T.wn[:], T.wnv[:]), "lwn", 16)
+
+    def product(h, half, key, deps):
+        wait("t", *deps)
+        return run("t", g.tensor.matmul_mx(T.ps[:, 512 * h:512 * h + 256], T.wq[:, 128 * h:128 * h + 128], T.wp[:, 128 * h:128 * h + 128],
+                                           T.pq[:, 256 * half:256 * half + 256], T.pp[:, 256 * half:256 * half + 256], True, True), key)
+
+    def drain(h, half, key, k):
+        o = 512 * h + 256 * half
+        return S(T.res[:, o:o + 256], T.ps[:, 512 * h:512 * h + 256], deps=[k], key=key)
+    wait("t", ("kwq0", 1), ("kwq1", 1), kpsr, ("lown", 32), ("cqA", 2 * nA))
+    da = [drain(h, cls, "da%d" % h, product(h, cls, "ma%d" % h, [])) for h in range(8)]
+    wait("t", ("cqB", 2 * nB))
+    db = [drain(h, 1 - cls, "db%d" % h, product(h, 1 - cls, "mb%d" % h, [da[h]])) for h in range(8)]
+
+    wait("v", toff)
+    acc, out, prev = None, T.ya, T.yb
+    for h in range(8):
+        w = T.res[:, 512 * h:512 * h + 512].indirect(T.off[:, 16 * h:16 * h + 16])
+        if h == 0:
+            acc = V("cp", out[:], w, deps=[da[h], db[h]])
+        else:
+            acc = V("tt", out[:], w, prev[:], A.add, deps=[acc, da[h], db[h]], key="ky" if h == 7 else None)
+        out, prev = prev, out
+    wait("y", acc)
+    run("y", g.sync.dma_start(T.y[:], prev[:]), "ly", 16)
+
+    wait("g", ("ly", 16), ("lwn", 16), ("loc", total["loc"]))
+    g.wait_ge(T.sem.cv, total["cv"])

@@ -5,62 +5,28 @@ N = 8
 CODES = "float8_e4m3fn_x4"
 ROW = 80
 WIN = 17 * ROW
-SCRATCH = {
-    "xb": ("sbuf", [128, 1024], "bfloat16"),
-    "usl": ("sbuf", [128, 32], "bfloat16"),
-    "zb": ("sbuf", [128, 560], "bfloat16"),
-    "pk": ("sbuf", [128, 512], "bfloat16"),
-    "wz": ("sbuf", [128, 4096], "bfloat16"),
-    "zq": ("sbuf", [128, 140], CODES), "zp": ("sbuf", [128, 140], "uint8"),
-    "xq": ("sbuf", [128, 384], CODES), "xp": ("sbuf", [128, 384], "uint8"),
-    "wq": ("sbuf", [128, 1024], CODES), "wp": ("sbuf", [128, 1024], "uint8"),
-    "oq": ("sbuf", [128, 128], CODES), "op": ("sbuf", [128, 128], "uint8"),
-    "pq": ("sbuf", [128, 512], CODES), "pp": ("sbuf", [128, 512], "uint8"),
-    "rq": ("sbuf", [128, 64], CODES), "rp": ("sbuf", [128, 64], "uint8"),
-    "rsc": ("sbuf", [128, 16], "float32"),
-    "pi": ("sbuf", [128, 1], "int32"), "pj": ("sbuf", [128, 4], "int32"), "pf": ("sbuf", [128, 4], "float32"),
-    "c64": ("sbuf", [128, 64], "float32"), "d64": ("sbuf", [128, 64], "float32"), "m4": ("sbuf", [128, 64], "float32"),
-    "msk": ("sbuf", [128, 64], "float32"), "mk2": ("sbuf", [128, 64], "float32"),
-    "v0": ("sbuf", [128, 256], "float32"), "val": ("sbuf", [128, 256], "float32"),
-    "pc0": ("sbuf", [128, 16], "float32"), "pc": ("sbuf", [128, 16], "float32"), "qr": ("sbuf", [128, 1], "float32"),
-    "one": ("sbuf", [128, 16], "float32"), "rm": ("sbuf", [128, 128], "float32"), "nr": ("sbuf", [128, 128], "float32"),
-    "k0": ("sbuf", [128, 128], "float32"), "k1": ("sbuf", [128, 128], "float32"), "prio": ("sbuf", [128, 128], "float32"),
-    "sm": ("sbuf", [128, 64], "float32"), "s32": ("sbuf", [128, 32], "float32"),
-    "sc": ("sbuf", [128, 128], "float32"), "repa": ("sbuf", [128, 64], "float32"), "repb": ("sbuf", [128, 64], "float32"),
-    "la": ("sbuf", [128, 64], "float32"), "la2": ("sbuf", [128, 32], "float32"), "la3": ("sbuf", [128, 16], "float32"),
-    "pen": ("sbuf", [128, 16], "float32"),
-    "cb": ("sbuf", [128, 64], "float32"), "cb2": ("sbuf", [128, 32], "float32"), "lose": ("sbuf", [128, 16], "float32"),
-    "tb": ("sbuf", [128, 32], "float32"), "tt": ("sbuf", [128, 32], "float32"), "ts": ("sbuf", [128, 32], "float32"),
-    "bt": ("sbuf", [128, 32], "float32"), "lp": ("sbuf", [128, 16], "float32"), "fo": ("sbuf", [128, 16], "float32"),
-    "offa": ("sbuf", [128, 16], "uint16"), "offb": ("sbuf", [128, 16], "uint16"),
-    "inv": ("sbuf", [128, WIN], "float32"), "mkd": ("sbuf", [128, 64], "float32"), "sel": ("sbuf", [128, 64], "float32"),
-    "m64": ("sbuf", [128, 64], "float32"), "m32": ("sbuf", [128, 32], "float32"), "m16": ("sbuf", [128, 16], "float32"),
-    "eq": ("sbuf", [128, 128], "float32"), "eqp": ("sbuf", [128, 128], "float32"),
-    "e64": ("sbuf", [128, 64], "float32"), "e32": ("sbuf", [128, 32], "float32"), "pv": ("sbuf", [128, 16], "float32"),
-    "wnv": ("sbuf", [128, 16], "float32"), "win": ("sbuf", [128, 128], "float32"), "win2": ("sbuf", [128, 128], "float32"),
-    "cum": ("sbuf", [128, 128], "float32"), "t2": ("sbuf", [128, 128], "float32"), "ts2": ("sbuf", [128, 128], "float32"),
-    "b2": ("sbuf", [128, 128], "float32"), "cu2": ("sbuf", [128, 128], "float32"), "pr": ("sbuf", [128, 128], "float32"),
-    "f64": ("sbuf", [128, 64], "float32"), "f32": ("sbuf", [128, 32], "float32"), "x1": ("sbuf", [128, 32], "float32"),
-    "t1": ("sbuf", [128, 32], "float32"), "off": ("sbuf", [128, 128], "uint16"),
-    "ps": ("psum", [128, 4096], "float32"),
-    "res": ("sbuf", [128, 4096], "float32"),
-    "ya": ("sbuf", [128, 256], "float32"), "yb": ("sbuf", [128, 256], "float32"),
-}
-SEMAPHORES = (["cv", "loc", "scA", "scB", "cqA", "cqB", "rs0", "rs1", "rs2",
+
+
+def sb(kind, **cols):
+    return {k: ("sbuf", [128, n], kind) for k, n in cols.items()}
+
+
+SCRATCH = {"ps": ("psum", [128, 4096], "float32")}
+SCRATCH.update(sb("bfloat16", xb=1024, usl=32, zb=560, pk=512, wz=4096, zz=512))
+SCRATCH.update(sb(CODES, zq=140, xq=384, wq=1024, oq=128, pq=512, rq=64))
+SCRATCH.update(sb("uint8", zp=140, xp=384, wp=1024, op=128, pp=512, rp=64))
+SCRATCH.update(sb("int32", pi=1, pj=4))
+SCRATCH.update(sb("float32", pf=4, c64=64, d64=64, m4=64, msk=64, mk2=64, v0=256, val=256, pc0=16, pc=16, qr=1, one=16,
+                  rm=128, k8=8, prio=128))
+SCRATCH.update(sb("float32", rsc=16, sm=64, s32=32, sc=128, repa=64, repb=64, la=64, la2=32, la3=16, pen=16, cb=64, cb2=32,
+                  lose=16, tb=32, tt=32, ts=32, bt=32, lp=16, fo=16, inv=WIN, mkd=64, sel=64))
+SCRATCH.update(sb("uint16", offa=16, offb=16, off=128))
+SCRATCH.update(sb("float32", m64=64, m32=32, m16=16, eq=128, eqp=128, e64=64, e32=32, pv=16, wnv=16, win=128, win2=128, cum=128,
+                  t2=128, ts2=128, b2=128, bk=8, cu2=128, pr=128, f64=64, f32=32, x1=32, t1=64, res=4096, ya=256, yb=256))
+SEMAPHORES = (["cv", "cw", "loc", "scA", "scB", "cqA", "cqB", "rs0", "rs1", "rs2",
                "lus", "lx", "lw0", "lw1", "lown", "lwn", "ly",
-               "kz", "kzs", "kzq", "kxp", "kxq", "ksc", "ksr", "kps", "kpsr", "kio", "kw0", "kw1", "kwq0", "kwq1", "kpk", "kwn", "ky"]
-              + ["%s%d" % (k, h) for k in ("ma", "da", "mb", "db") for h in range(8)])
-
-
-def roads(core, T, topo):
-    others = [c for c in T.cores if c != core]
-    near = [c for c in others if topo.may_write(core, c)]
-    far = [c for c in others if not topo.may_write(core, c)]
-    help_ = [c for c in topo.cores_of(core) if c not in T.cores and all(topo.may_write(c, d) for d in far)]
-    help_.sort(key=lambda c: topo.die(c) == topo.die(core))
-    help_ = help_[:2]
-    share = {h: far[k::len(help_)] for k, h in enumerate(help_)}
-    return near, far, help_, share
+               "kz", "kzz", "kzs", "kzq", "kxp", "kxq", "ksc", "ksr", "kps", "kpsr", "kio", "kw0", "kw1", "kwv", "kwq0", "kwq1",
+               "kpk", "kwn", "kwin", "kw2", "ky0", "ky1"] + ["%s%d" % (k, h) for k in ("ma", "da", "mb", "db") for h in range(8)])
 
 
 def order(T, topo):
@@ -68,33 +34,64 @@ def order(T, topo):
     return [a, [c for c in T.cores if c not in a]]
 
 
+def roads(core, T, topo):
+    two = order(T, topo)
+    own, far = two if core in two[0] else two[::-1]
+    near = [c for c in own if c != core]
+    cand = [c for c in topo.cores_of(core) if c not in T.cores and all(topo.may_write(c, d) for d in far)]
+    a = [c for c in cand if topo.die(c) != topo.die(core)]
+    b = [c for c in cand if topo.die(c) == topo.die(core)]
+    hc, hp = [a[0], b[0]], [a[1], b[1]]
+    k = own.index(core)
+    codes = {h: [d for j, d in enumerate(far) if (j + k) % 2 == i] for i, h in enumerate(hc)}
+    planes = {h: [d for j, d in enumerate(far) if (j + k) % 2 == i] + [d for j, d in enumerate(near) if (j + k) % 2 == i]
+              for i, h in enumerate(hp)}
+    scores = {h: [d for j, d in enumerate(far) if (j + k) % 4 == i] for i, h in enumerate(hc + hp)}
+    return near, far, codes, planes, scores
+
+
 def bits(engines):
     return sum(1 << e for e in engines)
 
 
-def ids(core, dests, topo):
-    r = []
-    for d in dests:
-        rid, pid = topo.addr(d, core)
-        r.append(DstId(rid=rid, pnc=pid))
-    return r
+def write(g, core, dests, engines, src, dst, sems, T, topo):
+    groups = [(s, [d for d, e in zip(dests, sems) if e == s]) for s in sorted(set(sems))]
+    n = len(engines) // len(groups)
+    tr = []
+    for k, (s, ds) in enumerate(groups):
+        i = []
+        for d in ds:
+            rid, pid = topo.addr(d, core)
+            i.append(DstId(rid=rid, pnc=pid))
+        tr.append(RemoteDMATransfer(dst_ids=i, dma_engine_mask=bits(engines[k * n:(k + 1) * n]), remote_sem=T.sem[s],
+                                    srcs=[src], dsts=[dst] * len(ds)))
+    g.remote_dma_fused(tr, local_sem=T.sem.loc)
+    return n * len(groups)
 
 
-def relay(g, core, boss, dests, T, topo):
+def engines_of(core, near, helper, topo):
+    off, every = topo.engines(core, near), topo.engines(core, helper)
+    return off, [e for e in every if e not in off], every
+
+
+def relay(g, core, boss, T, topo):
+    near, far, codes, planes, scores = roads(boss, T, topo)
+    if core not in scores:
+        return
     p = sum(order(T, topo), []).index(boss)
-    eng = topo.engines(core, dests[0])
-
-    def send(src, dst, sem):
-        g.remote_dma_fused([RemoteDMATransfer(dst_ids=ids(core, dests, topo), dma_engine_mask=bits(eng), remote_sem=sem,
-                                              srcs=[src], dsts=[dst] * len(dests))], local_sem=T.sem.loc)
-    k = len([e for e in topo.engines(boss, core) if e not in eng])
-    g.wait_ge(T.sem.rs0, k)
-    send(T.rsc[:], T.sc[:, 16 * p:16 * p + 16], T.sem.scB)
-    g.wait_ge(T.sem.rs1, k)
-    send(T.rq[:].bitcast(dt.uint8), T.pq[:, 64 * p:64 * p + 64].bitcast(dt.uint8), T.sem.cqB)
-    g.wait_ge(T.sem.rs2, k)
-    send(T.rp[:], T.pp[:, 64 * p:64 * p + 64], T.sem.cqB)
-    g.wait_ge(T.sem.loc, 3 * len(eng))
+    eng = topo.engines(core, far[0])
+    _, eon, every = engines_of(boss, near[0], core, topo)
+    g.wait_ge(T.sem.rs0, len(eon))
+    n = write(g, core, scores[core], eng, T.rsc[:], T.sc[:, 16 * p:16 * p + 16], ["scB"] * len(scores[core]), T, topo)
+    if core in codes:
+        g.wait_ge(T.sem.rs1, len(every))
+        n += write(g, core, codes[core], eng, T.rq[:].bitcast(dt.uint8), T.pq[:, 64 * p:64 * p + 64].bitcast(dt.uint8),
+                   ["cqB"] * len(codes[core]), T, topo)
+    else:
+        g.wait_ge(T.sem.rs2, len(every))
+        n += write(g, core, planes[core], eng, T.rp[:], T.pp[:, 64 * p:64 * p + 64],
+                   ["cqA" if d in near else "cqB" for d in planes[core]], T, topo)
+    g.wait_ge(T.sem.loc, n)
 
 
 def rank_program(g, core, T, topo):
@@ -102,16 +99,14 @@ def rank_program(g, core, T, topo):
     if rank is None:
         for boss in T.cores:
             if core in topo.cores_of(boss):
-                share = roads(boss, T, topo)[3]
-                if core in share:
-                    relay(g, core, boss, share[core], T, topo)
+                relay(g, core, boss, T, topo)
         return
-    near, far, helpers, share = roads(core, T, topo)
-    planes = order(T, topo)
-    pieces = planes[0] + planes[1]
-    cls = 0 if core in planes[0] else 1
+    near, far, hcodes, hplanes, hscores = roads(core, T, topo)
+    two = order(T, topo)
+    pieces = two[0] + two[1]
+    cls = 0 if core in two[0] else 1
     mine = pieces.index(core)
-    idx = planes[cls].index(core)
+    idx = two[cls].index(core)
     rk = [T.rank_of(c) for c in pieces]
 
     Q = {"v": [g.vector, "cv"], "s": [g.scalar, None], "t": [g.tensor, None], "g": [g, None], "y": [g.sync, None]}
@@ -123,7 +118,7 @@ def rank_program(g, core, T, topo):
             if d is None:
                 continue
             sem, val = d
-            if sem == Q[q][1]:
+            if sem in ("cv", "cw"):
                 val = total[sem]
             if seen[q].get(sem, 0) < val:
                 Q[q][0].wait_ge(T.sem[sem], val)
@@ -155,11 +150,19 @@ def rank_program(g, core, T, topo):
     iota(T.c64[:], [[1, 4], [0, 16]], 0, 0)
     iota(T.d64[:], [[0, 16], [1, 4]], 0, 0)
     iota(T.pc0[:], [[1, 16]], 0, 0)
-    iota(T.k0[:], [[64, 8], [0, 16]], -1, 0)
+    iota(T.k8[:], [[64, 8]], -1, 0)
     kio = iota(T.v0[:], [[4, 16], [64, 16]], 0, 0)
 
+    kzz = V("set", T.zz[:], 0.0, key="kzz")
     kz = V("set", T.zb[:], 0.0, key="kz")
     zpk = V("set", T.pk[:], 0.0)
+    V("set", T.la[:, 16 * idx:16 * idx + 16], 0.0)
+    V("set", T.one[:], 1.0)
+    V("set", T.rm[:], 1.0)
+    V("set", T.tb[:], 0.0)
+    V("set", T.ts[:], 0.0)
+    V("set", T.ts2[:, 0:1], 0.0)
+    V("set", T.inv[:, 0:64], 0.0)
     kxp = V("q", T.xq[:, 256:384], T.xp[:, 256:384], T.pk[:], deps=[zpk], key="kxp")
     wait("v", kio)
     V("ts", T.pj[:, 0:1], T.pi[:], 3, None, A.bitwise_and)
@@ -168,6 +171,11 @@ def rank_program(g, core, T, topo):
     t = V("cp", T.pf[:, 0:3], T.pj[:, 0:3], deps=[t])
     pt, pa, pqq = T.pf[:, 0:1], T.pf[:, 1:2], T.pf[:, 2:3]
     V("ts", T.msk[:], T.c64[:], pt, None, A.is_equal, deps=[t])
+
+    def zero(block, key):
+        return S(T.wz[:, 512 * block:512 * block + 512], T.zz[:], deps=[kzz], key=key)
+    zero(0, "kw0")
+    zero(1, "kw0")
     zs = ksz = None
     for l in range(4):
         for e in range(4):
@@ -178,8 +186,11 @@ def rank_program(g, core, T, topo):
             else:
                 ksz = S(o, i, deps=[kz, lus], key="kzs")
     kzq = V("q", T.zq[:], T.zp[:], T.zb[:], deps=[zs, ksz], key="kzq")
-    kw0 = V("set", T.wz[:, 0:2048], 0.0, key="kw0")
     kxq = V("q", T.xq[:, 0:256], T.xp[:, 0:256], T.xb[:], deps=[lx], key="kxq")
+    zero(2, "kw0")
+    kw0 = zero(3, "kw0")
+    zero(4, "kw1")
+    kw1 = zero(5, "kw1")
 
     wait("t", kzq, kxp, kxq)
     for i in range(4):
@@ -191,42 +202,44 @@ def rank_program(g, core, T, topo):
     own = T.sc[:, 16 * mine:16 * mine + 16]
     ksc = V("tt", own, T.s32[:, 0:16], T.s32[:, 16:32], A.add, deps=[t], key="ksc")
 
-    eoff = topo.engines(core, near[0])
-    eon = [e for e in topo.engines(core, helpers[0]) if e not in eoff]
-
-    def send(src, dst, hop, sem, hsem):
-        g.remote_dma_fused([
-            RemoteDMATransfer(dst_ids=ids(core, helpers, topo), dma_engine_mask=bits(eon), remote_sem=T.sem[hsem],
-                              srcs=[src], dsts=[hop] * len(helpers)),
-            RemoteDMATransfer(dst_ids=ids(core, near, topo), dma_engine_mask=bits(eoff), remote_sem=T.sem[sem],
-                              srcs=[src], dsts=[dst] * len(near))], local_sem=T.sem.loc)
-        total["loc"] = total.get("loc", 0) + len(eon) + len(eoff)
-    wait("g", ksc)
-    send(own, own, T.rsc[:], "scA", "rs0")
+    hs = list(hscores)
+    eoff, eon, every = engines_of(core, near[0], hs[0], topo)
     nA = len(near) * len(eoff)
-    nB = sum(len(topo.engines(roads(c, T, topo)[2][0], core)) for c in far)
+    nB = sum(len(topo.engines(h, core)) for c in far for h, d in roads(c, T, topo)[4].items() if core in d)
+
+    def arriving(c):
+        r = roads(c, T, topo)
+        n = len(eoff) if core in r[0] else sum(len(topo.engines(h, core)) for h, d in r[2].items() if core in d)
+        for h, d in r[3].items():
+            if core in d:
+                e = len(topo.engines(h, core))
+                n += e // (2 if any(x in r[0] for x in d) and any(x in r[1] for x in d) else 1)
+        return n
+    wait("g", ksc)
+    loc = write(g, core, hs, eon, own, T.rsc[:], ["rs0"] * len(hs), T, topo)
+    loc += write(g, core, near, eoff, own, own, ["scA"] * len(near), T, topo)
 
     ksr = None
     for i in range(4):
         ksr = S(T.repa[:, 16 * i:16 * i + 16], own, deps=[ksc], key="ksr")
-    kw1 = V("set", T.wz[:, 2048:4096], 0.0, key="kw1")
-    for half, kw in ((0, kw0), (1, kw1)):
-        wait("y", kw)
+    kwv = V("set", T.wz[:, 3072:4096], 0.0, key="kwv")
+    for half, kw in enumerate(([kw0], [kw1, kwv])):
+        wait("y", *kw)
         for h in range(4 * half, 4 * half + 4):
             run("y", g.sync.dma_start(T.wz[16 * h:16 * h + 16, 512 * h:512 * h + 512], T.w[16 * h:16 * h + 16, :]), "lw%d" % half, 16)
-    V("set", T.la[:, 16 * idx:16 * idx + 16], 0.0)
-    V("set", T.one[:], 1.0)
-    t = V("set", T.rm[:], 1.0)
-    V("set", T.tb[:], 0.0)
-    V("set", T.ts[:], 0.0)
-    V("set", T.ts2[:, 0:1], 0.0)
-    V("set", T.inv[:, 0:64], 0.0)
+
+    def wquant(half):
+        V("q", T.wq[:, 512 * half:512 * half + 512], T.wp[:, 512 * half:512 * half + 512],
+          T.wz[:, 2048 * half:2048 * half + 2048], deps=[("lw%d" % half, 64)], key="kwq%d" % half)
+    V("set", T.rm[:, 0:128:16], 0.0)
     t2 = V("ts", T.qr[:], pqq, float(ROW), float(ROW + 1), A.mult, A.add)
     V("ts", T.m4[:], T.d64[:], 1.0, None, A.min)
     V("ts", T.mk2[:], T.d64[:], pa, None, A.is_equal)
     V("ts", T.val[:], T.v0[:], pt, None, A.add)
-    V("set", T.rm[:, 0:128:16], 0.0, deps=[t])
     V("ts", T.pc[:], T.pc0[:], T.qr[:], None, A.add, deps=[t2])
+    for i in range(8):
+        V("set", T.prio[:, 16 * i:16 * i + 16], float(8 - rk[i]))
+    wquant(0)
 
     ca, cb = 64 * cls, 64 * (1 - cls)
     wait("v", ksr, ("scA", nA), ksc)
@@ -240,13 +253,10 @@ def rank_program(g, core, T, topo):
     t = V("ts", T.pen[:], T.la3[:], -1e28, None, A.mult, deps=[t])
     for i in range(4):
         tr = V("tt", T.repb[:, 16 * i:16 * i + 16], own, T.pen[:], A.add, deps=[t] if i == 0 else [])
-    for half in range(2):
-        wait("v", ("lw%d" % half, 64))
-        V("q", T.wq[:, 512 * half:512 * half + 512], T.wp[:, 512 * half:512 * half + 512],
-          T.wz[:, 2048 * half:2048 * half + 2048], key="kwq%d" % half)
+    wquant(1)
 
     wait("v", tr, ("scB", nB))
-    low = 16 * len([c for c in planes[1 - cls] if T.rank_of(c) < rank])
+    low = 16 * len([c for c in far if T.rank_of(c) < rank])
     if low > 0:
         t = V("tt", T.cb[:, 0:low], T.sc[:, cb:cb + low], T.repb[:, 0:low], A.is_ge)
     if low < 64:
@@ -254,12 +264,12 @@ def rank_program(g, core, T, topo):
     t = V("tt", T.cb2[:], T.cb[:, 0:32], T.cb[:, 32:64], A.max, deps=[t])
     t = V("tt", T.lose[:], T.cb2[:, 0:16], T.cb2[:, 16:32], A.max, deps=[t])
     t = V("scan", T.tb[:, 0:16], T.one[:], T.lose[:], -1.0, A.add, A.subtract, deps=[t])
-    V("tt", T.lp[:], T.lose[:], T.pc[:], A.mult)
+    tw = V("tt", T.lp[:], T.lose[:], T.pc[:], A.mult, key="cw")
     t = V("tr", T.tt[:], T.tb[:], deps=[t])
-    V("tt", T.fo[:], T.tb[:, 0:16], T.lp[:], A.add)
+    tw = V("tt", T.fo[:], T.tb[:, 0:16], T.lp[:], A.add, deps=[tw], key="cw")
     t = V("scan", T.ts[:, 1:32], T.tt[:, 0:31], T.rm[:, 1:32], 0.0, A.add, A.mult, deps=[t])
     t = V("tr", T.bt[:], T.ts[:], deps=[t])
-    t = V("ts", T.offa[:], T.fo[:], T.bt[:, 15:16], pqq, A.add, A.add, deps=[t])
+    t = V("ts", T.offa[:], T.fo[:], T.bt[:, 15:16], pqq, A.add, A.add, deps=[t, tw])
     t = V("cp", T.inv[:, 0:WIN].indirect(T.offa[:, 0:16]), T.val[:], deps=[t])
     t = V("tt", T.mkd[:], T.inv[:, 0:64], T.mk2[:], A.mult, deps=[t])
     t = V("scan", T.sel[:], T.m4[:], T.mkd[:], 0.0, A.mult, A.add, deps=[t])
@@ -267,19 +277,20 @@ def rank_program(g, core, T, topo):
     t = V("cp", T.pk[:, 0:256], T.xb[:, 0:1024].indirect(T.offb[:, 0:16]), deps=[t])
     kpk = V("q", T.oq[:], T.op[:], T.pk[:], deps=[t], key="kpk")
 
-    wait("g", kpk)
     c0 = 64 * mine
-    send(T.oq[:, 0:64].bitcast(dt.uint8), T.pq[:, c0:c0 + 64].bitcast(dt.uint8), T.rq[:].bitcast(dt.uint8), "cqA", "rs1")
-    send(T.op[:, 0:64], T.pp[:, c0:c0 + 64], T.rp[:], "cqA", "rs2")
+    oq, pq = T.oq[:, 0:64].bitcast(dt.uint8), T.pq[:, c0:c0 + 64].bitcast(dt.uint8)
+    op, pp = T.op[:, 0:64], T.pp[:, c0:c0 + 64]
+    wait("g", kpk)
+    loc += write(g, core, list(hcodes), every, oq, T.rq[:].bitcast(dt.uint8), ["rs1"] * len(hcodes), T, topo)
+    loc += write(g, core, list(hplanes), every, op, T.rp[:], ["rs2"] * len(hplanes), T, topo)
+    loc += write(g, core, near, eoff, oq, pq, ["cqA"] * len(near), T, topo)
     wait("y", kpk)
-    run("y", g.sync.dma_start(T.pq[:, c0:c0 + 64].bitcast(dt.uint8), T.oq[:, 0:64].bitcast(dt.uint8)), "lown", 16)
-    run("y", g.sync.dma_start(T.pp[:, c0:c0 + 64], T.op[:, 0:64]), "lown", 16)
+    run("y", g.sync.dma_start(pq, oq), "lown", 16)
+    run("y", g.sync.dma_start(pp, op), "lown", 16)
 
     t = V("tt", T.m64[:], T.sc[:, 0:64], T.sc[:, 64:128], A.max)
     t = V("tt", T.m32[:], T.m64[:, 0:32], T.m64[:, 32:64], A.max, deps=[t])
     t = V("tt", T.m16[:], T.m32[:, 0:16], T.m32[:, 16:32], A.max, deps=[t])
-    for i in range(8):
-        V("set", T.prio[:, 16 * i:16 * i + 16], float(8 - rk[i]))
     for i in range(8):
         t = V("tt", T.eq[:, 16 * i:16 * i + 16], T.sc[:, 16 * i:16 * i + 16], T.m16[:], A.is_equal, deps=[t] if i == 0 else [])
     t = V("tt", T.eqp[:], T.eq[:], T.prio[:], A.mult, deps=[t])
@@ -287,26 +298,29 @@ def rank_program(g, core, T, topo):
     t = V("tt", T.e32[:], T.e64[:, 0:32], T.e64[:, 32:64], A.max, deps=[t])
     t = V("tt", T.pv[:], T.e32[:, 0:16], T.e32[:, 16:32], A.max, deps=[t])
     for i in range(8):
-        t = V("ts", T.win[:, 16 * i:16 * i + 16], T.pv[:], float(8 - rk[i]), None, A.is_equal, deps=[t] if i == 0 else [])
-    t = V("scan", T.cum[:], T.rm[:], T.win[:], 0.0, A.mult, A.add, deps=[t])
-    V("ts", T.nr[:], T.rm[:], -1.0, 1.0, A.mult, A.add)
+        kwin = V("ts", T.win[:, 16 * i:16 * i + 16], T.pv[:], float(8 - rk[i]), None, A.is_equal, deps=[t] if i == 0 else [], key="kwin")
+    kw2 = S(T.win2[:], T.win[:], deps=[kwin], key="kw2")
+    t = V("scan", T.cum[:], T.rm[:], T.win[:], 0.0, A.mult, A.add, deps=[kwin])
     kwn = V("ts", T.wnv[:], T.pv[:], -1.0, 8.0, A.mult, A.add, key="kwn")
     t = V("tr", T.t2[:], T.cum[:], deps=[t])
-    V("tt", T.k1[:], T.k0[:], T.nr[:], A.mult)
     t = V("scan", T.ts2[:, 1:128], T.t2[:, 0:127], T.rm[:, 1:128], 0.0, A.add, A.mult, deps=[t])
-    V("tt", T.win2[:], T.win[:], T.k1[:], A.add)
     t = V("tr", T.b2[:], T.ts2[:], deps=[t])
-    t = V("tt", T.win2[:, 0:128:16], T.win2[:, 0:128:16], T.b2[:, 15:128:16], A.add, deps=[t])
+    t = V("tt", T.bk[:], T.b2[:, 15:128:16], T.k8[:], A.add, deps=[t])
+    t = V("tt", T.win2[:, 0:128:16], T.win2[:, 0:128:16], T.bk[:], A.add, deps=[t, kw2])
     t = V("scan", T.cu2[:], T.rm[:], T.win2[:], 0.0, A.mult, A.add, deps=[t])
     t = V("tt", T.pr[:], T.cu2[:], T.win[:], A.mult, deps=[t])
     t = V("tt", T.f64[:], T.pr[:, 0:64], T.pr[:, 64:128], A.add, deps=[t])
     t = V("tt", T.f32[:], T.f64[:, 0:32], T.f64[:, 32:64], A.add, deps=[t])
     V("tt", T.x1[:, 0:16], T.f32[:, 0:16], T.f32[:, 16:32], A.add, deps=[t])
     t = V("tt", T.x1[:, 16:32], T.f32[:, 0:16], T.f32[:, 16:32], A.add)
-    t = V("tr", T.t1[:], T.x1[:], deps=[t])
-    for a in range(4):
+    V("tr", T.t1[0:64, 0:32], T.x1[0:64, :], deps=[t])
+    t = V("tr", T.t1[64:128, 32:64], T.x1[64:128, :])
+    V("cp", T.t1[64:128, 0:32], T.t1[0:64, 0:32], deps=[t])
+    t = V("cp", T.t1[0:64, 32:64], T.t1[64:128, 32:64])
+    for e in range(2):
         for b in range(4):
-            t = V("cp", T.off[32 * b:32 * b + 32, 32 * a:32 * a + 32], T.t1[32 * a:32 * a + 32, 0:32], deps=[t] if a + b == 0 else [])
+            a = b // 2 * 2 + e
+            t = V("cp", T.off[32 * b:32 * b + 32, 64 * e:64 * e + 64], T.t1[32 * a:32 * a + 32, 0:64], deps=[t] if e + b == 0 else [])
     toff = t
     wait("y", kwn)
     run("y", g.sync.dma_start(T.wn[:], T.wnv[:]), "lwn", 16)
@@ -319,22 +333,25 @@ def rank_program(g, core, T, topo):
     def drain(h, half, key, k):
         o = 512 * h + 256 * half
         return S(T.res[:, o:o + 256], T.ps[:, 512 * h:512 * h + 256], deps=[k], key=key)
-    wait("t", ("kwq0", 1), ("kwq1", 1), kpsr, ("lown", 32), ("cqA", 2 * nA))
+    wait("t", ("kwq0", 1), ("kwq1", 1), kpsr, ("lown", 32), ("cqA", sum(arriving(c) for c in near)))
     da = [drain(h, cls, "da%d" % h, product(h, cls, "ma%d" % h, [])) for h in range(8)]
-    wait("t", ("cqB", 2 * nB))
+    wait("t", ("cqB", sum(arriving(c) for c in far)))
     db = [drain(h, 1 - cls, "db%d" % h, product(h, 1 - cls, "mb%d" % h, [da[h]])) for h in range(8)]
 
-    wait("v", toff)
-    acc, out, prev = None, T.ya, T.yb
-    for h in range(8):
-        w = T.res[:, 512 * h:512 * h + 512].indirect(T.off[:, 16 * h:16 * h + 16])
-        if h == 0:
-            acc = V("cp", out[:], w, deps=[da[h], db[h]])
-        else:
-            acc = V("tt", out[:], w, prev[:], A.add, deps=[acc, da[h], db[h]], key="ky" if h == 7 else None)
+    def found(h, a, b):
+        o = 64 * (h // 2 % 2) + 32 * (h // 4) + 16 * (h % 2)
+        return T.res[:, 512 * h:512 * h + 512].indirect(T.off[:, o + a // 16:o + b // 16])
+    out, prev = T.ya, T.yb
+    acc = V("cp", out[:], found(0, 0, 256), deps=[toff, da[0], db[0]])
+    for h in range(1, 7):
         out, prev = prev, out
-    wait("y", acc)
-    run("y", g.sync.dma_start(T.y[:], prev[:]), "ly", 16)
+        acc = V("tt", out[:], found(h, 0, 256), prev[:], A.add, deps=[acc, da[h], db[h]])
+    out, prev = prev, out
+    for i, q in enumerate(("y", "s")):
+        a, b = 128 * i, 128 * i + 128
+        k = V("tt", out[:, a:b], found(7, a, b), prev[:, a:b], A.add, deps=[acc, da[7], db[7]], key="ky%d" % i)
+        wait(q, k)
+        run(q, Q[q][0].dma_start(T.y[:, a:b], out[:, a:b]), "ly", 16)
 
-    wait("g", ("ly", 16), ("lwn", 16), ("loc", total["loc"]))
+    wait("g", ("ly", 32), ("lwn", 16), ("loc", loc))
     g.wait_ge(T.sem.cv, total["cv"])

@@ -5,6 +5,7 @@ N = 8
 CODES = "float8_e4m3fn_x4"
 ROW = 80
 WIN = 17 * ROW
+FIRST = 3
 
 
 def sb(kind, **cols):
@@ -17,15 +18,16 @@ SCRATCH.update(sb(CODES, zq=140, xq=384, wq=1024, oq=128, pq=512, rq=64))
 SCRATCH.update(sb("uint8", zp=140, xp=384, wp=1024, op=128, pp=512, rp=64))
 SCRATCH.update(sb("int32", pi=1, pj=4))
 SCRATCH.update(sb("float32", pf=4, c64=64, d64=64, m4=64, msk=64, mk2=64, v0=256, val=256, pc0=16, pc=16, qr=1, one=16,
-                  rm=128, k8=8, prio=128))
+                  rm=128, k8=8, prio=128, rc=8))
 SCRATCH.update(sb("float32", rsc=16, sm=64, s32=32, sc=128, repa=64, repb=64, la=64, la2=32, la3=16, pen=16, cb=64, cb2=32,
                   lose=16, tb=32, tt=32, ts=32, bt=32, lp=16, fo=16, inv=WIN, mkd=64, sel=64))
 SCRATCH.update(sb("uint16", offa=16, offb=16, off=128))
-SCRATCH.update(sb("float32", m64=64, m32=32, m16=16, eq=128, eqp=128, e64=64, e32=32, pv=16, wnv=16, win=128, win2=128, cum=128,
+SCRATCH.update(sb("float32", m64=64, m32=32, m16=32, eq=128, eqp=128, e64=64, e32=32, pv=32, wnv=16, win=128, win2=128, cum=128,
                   t2=128, ts2=128, b2=128, bk=8, cu2=128, pr=128, f64=64, f32=32, x1=32, t1=64, res=4096, ya=256, yb=256))
-SEMAPHORES = (["cv", "cw", "loc", "scA", "scB", "cqA", "cqB", "rs0", "rs1", "rs2",
+SEMAPHORES = (["cv", "cw", "loc", "scA", "scB", "cqA", "cqB", "rs0", "rs1", "rs2", "kc",
                "lus", "lx", "lw0", "lw1", "lown", "lwn", "ly",
-               "kz", "kzz", "kzs", "kzq", "kxp", "kxq", "ksc", "ksr", "kps", "kpsr", "kio", "kw0", "kw1", "kwv", "kwq0", "kwq1",
+               "kz", "kzz", "kzs", "kzq", "kxp", "kxq", "ksc", "ksr", "kps", "kpsr", "kio", "kio0", "kpf", "kpz", "kval",
+               "kpr", "kw0", "kw1", "kwq0", "kwq1",
                "kpk", "kwn", "kwin", "kw2", "ky0", "ky1"] + ["%s%d" % (k, h) for k in ("ma", "da", "mb", "db") for h in range(8)])
 
 
@@ -44,29 +46,25 @@ def roads(core, T, topo):
     hc, hp = [a[0], b[0]], [a[1], b[1]]
     k = own.index(core)
     codes = {h: [d for j, d in enumerate(far) if (j + k) % 2 == i] for i, h in enumerate(hc)}
-    planes = {h: [d for j, d in enumerate(far) if (j + k) % 2 == i] + [d for j, d in enumerate(near) if (j + k) % 2 == i]
-              for i, h in enumerate(hp)}
+    planes = {h: [d for j, d in enumerate(far) if (j + k) % 2 == i] for i, h in enumerate(hp)}
+    nplanes = dict(zip(hc + [hp[k % 2]], [[d] for d in near]))
     scores = {h: [d for j, d in enumerate(far) if (j + k) % 4 == i] for i, h in enumerate(hc + hp)}
-    return near, far, codes, planes, scores
+    return {"near": near, "far": far, "codes": codes, "planes": planes, "nplanes": nplanes, "scores": scores,
+            "handed": hp + [h for h in hc if h in nplanes]}
 
 
 def bits(engines):
     return sum(1 << e for e in engines)
 
 
-def write(g, core, dests, engines, src, dst, sems, T, topo):
-    groups = [(s, [d for d, e in zip(dests, sems) if e == s]) for s in sorted(set(sems))]
-    n = len(engines) // len(groups)
-    tr = []
-    for k, (s, ds) in enumerate(groups):
-        i = []
-        for d in ds:
-            rid, pid = topo.addr(d, core)
-            i.append(DstId(rid=rid, pnc=pid))
-        tr.append(RemoteDMATransfer(dst_ids=i, dma_engine_mask=bits(engines[k * n:(k + 1) * n]), remote_sem=T.sem[s],
-                                    srcs=[src], dsts=[dst] * len(ds)))
-    g.remote_dma_fused(tr, local_sem=T.sem.loc)
-    return n * len(groups)
+def write(g, core, dests, engines, src, dst, sem, T, topo):
+    i = []
+    for d in dests:
+        rid, pid = topo.addr(d, core)
+        i.append(DstId(rid=rid, pnc=pid))
+    g.remote_dma_fused([RemoteDMATransfer(dst_ids=i, dma_engine_mask=bits(engines), remote_sem=T.sem[sem],
+                                          srcs=[src], dsts=[dst] * len(i))], local_sem=T.sem.loc)
+    return len(engines)
 
 
 def engines_of(core, near, helper, topo):
@@ -75,22 +73,28 @@ def engines_of(core, near, helper, topo):
 
 
 def relay(g, core, boss, T, topo):
-    near, far, codes, planes, scores = roads(boss, T, topo)
-    if core not in scores:
+    r = roads(boss, T, topo)
+    if core not in r["scores"]:
         return
     p = sum(order(T, topo), []).index(boss)
-    eng = topo.engines(core, far[0])
-    _, eon, every = engines_of(boss, near[0], core, topo)
+    eng = topo.engines(core, r["far"][0])
+    _, eon, every = engines_of(boss, r["near"][0], core, topo)
+    half, what = list(r["scores"]).index(core) % 2, list(r["scores"]).index(core) // 2
+    step, base, buf = ((0, 1, T.one), (1, 8 * half, T.pc0))[what]
+    g.iota(T.rc[:], [[step, 8]], base, 0, allow_small_or_imprecise_dtypes=True).then_inc(T.sem.kio, 1)
+    g.wait_ge(T.sem.kio, 1)
+    n = write(g, core, [boss], eng, T.rc[:], buf[:, 8 * half:8 * half + 8], "kc", T, topo)
     g.wait_ge(T.sem.rs0, len(eon))
-    n = write(g, core, scores[core], eng, T.rsc[:], T.sc[:, 16 * p:16 * p + 16], ["scB"] * len(scores[core]), T, topo)
-    if core in codes:
+    n += write(g, core, r["scores"][core], eng, T.rsc[:], T.sc[:, 16 * p:16 * p + 16], "scB", T, topo)
+    if core in r["codes"]:
         g.wait_ge(T.sem.rs1, len(every))
-        n += write(g, core, codes[core], eng, T.rq[:].bitcast(dt.uint8), T.pq[:, 64 * p:64 * p + 64].bitcast(dt.uint8),
-                   ["cqB"] * len(codes[core]), T, topo)
-    else:
+        n += write(g, core, r["codes"][core], eng, T.rq[:].bitcast(dt.uint8), T.pq[:, 64 * p:64 * p + 64].bitcast(dt.uint8),
+                   "cqB", T, topo)
+    if core in r["handed"]:
         g.wait_ge(T.sem.rs2, len(every))
-        n += write(g, core, planes[core], eng, T.rp[:], T.pp[:, 64 * p:64 * p + 64],
-                   ["cqA" if d in near else "cqB" for d in planes[core]], T, topo)
+    for road, sem in (("planes", "cqB"), ("nplanes", "cqA")):
+        if core in r[road]:
+            n += write(g, core, r[road][core], eng, T.rp[:], T.pp[:, 64 * p:64 * p + 64], sem, T, topo)
     g.wait_ge(T.sem.loc, n)
 
 
@@ -101,7 +105,8 @@ def rank_program(g, core, T, topo):
             if core in topo.cores_of(boss):
                 relay(g, core, boss, T, topo)
         return
-    near, far, hcodes, hplanes, hscores = roads(core, T, topo)
+    road = roads(core, T, topo)
+    near, far = road["near"], road["far"]
     two = order(T, topo)
     pieces = two[0] + two[1]
     cls = 0 if core in two[0] else 1
@@ -136,41 +141,25 @@ def rank_program(g, core, T, topo):
              "scan": g.vector.tensor_tensor_scan, "tr": g.vector.transpose, "q": g.vector.quantize_mx}[name]
         return run("v", f(*args), key)
 
-    def S(out, in_, deps=(), key=None):
+    def S(out, in_, deps=(), key=None, **line):
         wait("s", *deps)
-        return run("s", g.scalar.activation(out, in_, ActivationFunctionType.Copy), key)
+        return run("s", g.scalar.activation(out, in_, ActivationFunctionType.Identity if line else ActivationFunctionType.Copy, **line), key)
 
-    def iota(out, pattern, base, cm):
-        return run("g", g.iota(out, pattern, base, cm, allow_small_or_imprecise_dtypes=True), "kio")
+    def iota(out, pattern, base, cm, key="kio"):
+        return run("g", g.iota(out, pattern, base, cm, allow_small_or_imprecise_dtypes=True), key)
 
     lus = run("y", g.sync.dma_start(T.usl[:], T.us[:, 0:32]), "lus", 16)
     lx = run("s", g.scalar.dma_start(T.xb[:], T.x[:]), "lx", 16)
 
-    iota(T.pi[:], [[0, 1]], 0, 1)
-    iota(T.c64[:], [[1, 4], [0, 16]], 0, 0)
+    iota(T.pi[:], [[0, 1]], 0, 1, "kio0")
+    kio0 = iota(T.c64[:], [[1, 4], [0, 16]], 0, 0, "kio0")
     iota(T.d64[:], [[0, 16], [1, 4]], 0, 0)
-    iota(T.pc0[:], [[1, 16]], 0, 0)
     iota(T.k8[:], [[64, 8]], -1, 0)
     kio = iota(T.v0[:], [[4, 16], [64, 16]], 0, 0)
 
     kzz = V("set", T.zz[:], 0.0, key="kzz")
     kz = V("set", T.zb[:], 0.0, key="kz")
-    zpk = V("set", T.pk[:], 0.0)
-    V("set", T.la[:, 16 * idx:16 * idx + 16], 0.0)
-    V("set", T.one[:], 1.0)
-    V("set", T.rm[:], 1.0)
-    V("set", T.tb[:], 0.0)
-    V("set", T.ts[:], 0.0)
-    V("set", T.ts2[:, 0:1], 0.0)
-    V("set", T.inv[:, 0:64], 0.0)
-    kxp = V("q", T.xq[:, 256:384], T.xp[:, 256:384], T.pk[:], deps=[zpk], key="kxp")
-    wait("v", kio)
-    V("ts", T.pj[:, 0:1], T.pi[:], 3, None, A.bitwise_and)
-    V("ts", T.pj[:, 1:2], T.pi[:], 2, 3, A.arith_shift_right, A.bitwise_and)
-    t = V("ts", T.pj[:, 2:3], T.pi[:], 15, None, A.bitwise_and)
-    t = V("cp", T.pf[:, 0:3], T.pj[:, 0:3], deps=[t])
-    pt, pa, pqq = T.pf[:, 0:1], T.pf[:, 1:2], T.pf[:, 2:3]
-    V("ts", T.msk[:], T.c64[:], pt, None, A.is_equal, deps=[t])
+    kxp = V("q", T.xq[:, 256:384], T.xp[:, 256:384], T.zz[:], deps=[kzz], key="kxp")
 
     def zero(block, key):
         return S(T.wz[:, 512 * block:512 * block + 512], T.zz[:], deps=[kzz], key=key)
@@ -190,56 +179,68 @@ def rank_program(g, core, T, topo):
     zero(2, "kw0")
     kw0 = zero(3, "kw0")
     zero(4, "kw1")
-    kw1 = zero(5, "kw1")
+    zero(5, "kw1")
+    wait("v", kio0)
+    V("ts", T.pj[:, 0:1], T.pi[:], 3, None, A.bitwise_and)
+    V("ts", T.pj[:, 1:2], T.pi[:], 2, 3, A.arith_shift_right, A.bitwise_and)
+    t = V("ts", T.pj[:, 2:3], T.pi[:], 15, None, A.bitwise_and)
+    kpf = V("cp", T.pf[:, 0:3], T.pj[:, 0:3], deps=[t], key="kpf")
+    pt, pa, pqq = T.pf[:, 0:1], T.pf[:, 1:2], T.pf[:, 2:3]
+    tm = V("ts", T.msk[:], T.c64[:], pt, None, A.is_equal, deps=[kpf])
 
     wait("t", kzq, kxp, kxq)
     for i in range(4):
         m = g.tensor.matmul_mx(T.ps[:, 0:128], T.zq[:, 12 - 4 * i:140 - 4 * i], T.zp[:, 12 - 4 * i:140 - 4 * i],
                                T.xq[:, 64 * i:64 * i + 128], T.xp[:, 64 * i:64 * i + 128], i == 0, i == 3)
     kps = run("t", m, "kps")
-    kpsr = V("tt", T.sm[:], T.ps[:, 0:64], T.msk[:], A.mult, deps=[kps], key="kpsr")
+    kpsr = V("tt", T.sm[:], T.ps[:, 0:64], T.msk[:], A.mult, deps=[kps, tm], key="kpsr")
     t = V("tt", T.s32[:], T.sm[:, 0:32], T.sm[:, 32:64], A.add, deps=[kpsr])
     own = T.sc[:, 16 * mine:16 * mine + 16]
     ksc = V("tt", own, T.s32[:, 0:16], T.s32[:, 16:32], A.add, deps=[t], key="ksc")
 
-    hs = list(hscores)
+    hs = list(road["scores"])
     eoff, eon, every = engines_of(core, near[0], hs[0], topo)
     nA = len(near) * len(eoff)
-    nB = sum(len(topo.engines(h, core)) for c in far for h, d in roads(c, T, topo)[4].items() if core in d)
+    theirs = {c: roads(c, T, topo) for c in near + far}
 
-    def arriving(c):
-        r = roads(c, T, topo)
-        n = len(eoff) if core in r[0] else sum(len(topo.engines(h, core)) for h, d in r[2].items() if core in d)
-        for h, d in r[3].items():
-            if core in d:
-                e = len(topo.engines(h, core))
-                n += e // (2 if any(x in r[0] for x in d) and any(x in r[1] for x in d) else 1)
-        return n
+    def arriving(c, *kinds):
+        return sum(len(topo.engines(h, core)) for k in kinds for h, d in theirs[c][k].items() if core in d)
+    nB = sum(arriving(c, "scores") for c in far)
+    kc = ("kc", sum(len(topo.engines(h, far[0])) for h in hs))
     wait("g", ksc)
-    loc = write(g, core, hs, eon, own, T.rsc[:], ["rs0"] * len(hs), T, topo)
-    loc += write(g, core, near, eoff, own, own, ["scA"] * len(near), T, topo)
+    loc = write(g, core, hs, eon, own, T.rsc[:], "rs0", T, topo)
+    loc += write(g, core, near, eoff, own, own, "scA", T, topo)
 
     ksr = None
     for i in range(4):
         ksr = S(T.repa[:, 16 * i:16 * i + 16], own, deps=[ksc], key="ksr")
-    kwv = V("set", T.wz[:, 3072:4096], 0.0, key="kwv")
-    for half, kw in enumerate(([kw0], [kw1, kwv])):
-        wait("y", *kw)
+    kpz = S(T.pk[:, 256:512], T.zz[:, 0:256], deps=[kzz], key="kpz")
+    zero(6, "kw1")
+    kw1 = zero(7, "kw1")
+    t = V("set", T.rm[:], 1.0)
+    V("set", T.la[:, 16 * idx:16 * idx + 16], 0.0)
+    V("set", T.tb[:], 0.0)
+    V("set", T.ts[:], 0.0)
+    V("set", T.ts2[:, 0:1], 0.0)
+    V("set", T.inv[:, 0:64], 0.0)
+    V("set", T.rm[:, 0:128:16], 0.0, deps=[t])
+    kval = S(T.val[:], T.v0[:], deps=[kio, kpf], key="kval", bias=pt)
+    for i in range(8):
+        kpr = S(T.prio[:, 16 * i:16 * i + 16], T.one[:], deps=[kc], key="kpr", scale=float(8 - rk[i]))
+    for half, kw in enumerate((kw0, kw1)):
+        wait("y", kw)
         for h in range(4 * half, 4 * half + 4):
             run("y", g.sync.dma_start(T.wz[16 * h:16 * h + 16, 512 * h:512 * h + 512], T.w[16 * h:16 * h + 16, :]), "lw%d" % half, 16)
 
     def wquant(half):
         V("q", T.wq[:, 512 * half:512 * half + 512], T.wp[:, 512 * half:512 * half + 512],
           T.wz[:, 2048 * half:2048 * half + 2048], deps=[("lw%d" % half, 64)], key="kwq%d" % half)
-    V("set", T.rm[:, 0:128:16], 0.0)
-    t2 = V("ts", T.qr[:], pqq, float(ROW), float(ROW + 1), A.mult, A.add)
+    wait("v", kio)
     V("ts", T.m4[:], T.d64[:], 1.0, None, A.min)
     V("ts", T.mk2[:], T.d64[:], pa, None, A.is_equal)
-    V("ts", T.val[:], T.v0[:], pt, None, A.add)
-    V("ts", T.pc[:], T.pc0[:], T.qr[:], None, A.add, deps=[t2])
-    for i in range(8):
-        V("set", T.prio[:, 16 * i:16 * i + 16], float(8 - rk[i]))
+    t = V("ts", T.qr[:], pqq, float(ROW), float(ROW + 1), A.mult, A.add)
     wquant(0)
+    V("ts", T.pc[:], T.pc0[:], T.qr[:], None, A.add, deps=[t, kc])
 
     ca, cb = 64 * cls, 64 * (1 - cls)
     wait("v", ksr, ("scA", nA), ksc)
@@ -263,45 +264,48 @@ def rank_program(g, core, T, topo):
         t = V("tt", T.cb[:, low:64], T.sc[:, cb + low:cb + 64], T.repb[:, low:64], A.is_gt)
     t = V("tt", T.cb2[:], T.cb[:, 0:32], T.cb[:, 32:64], A.max, deps=[t])
     t = V("tt", T.lose[:], T.cb2[:, 0:16], T.cb2[:, 16:32], A.max, deps=[t])
-    t = V("scan", T.tb[:, 0:16], T.one[:], T.lose[:], -1.0, A.add, A.subtract, deps=[t])
+    t = V("scan", T.tb[:, 0:16], T.one[:], T.lose[:], -1.0, A.add, A.subtract, deps=[t, kc])
     tw = V("tt", T.lp[:], T.lose[:], T.pc[:], A.mult, key="cw")
     t = V("tr", T.tt[:], T.tb[:], deps=[t])
     tw = V("tt", T.fo[:], T.tb[:, 0:16], T.lp[:], A.add, deps=[tw], key="cw")
     t = V("scan", T.ts[:, 1:32], T.tt[:, 0:31], T.rm[:, 1:32], 0.0, A.add, A.mult, deps=[t])
     t = V("tr", T.bt[:], T.ts[:], deps=[t])
-    t = V("ts", T.offa[:], T.fo[:], T.bt[:, 15:16], pqq, A.add, A.add, deps=[t, tw])
-    t = V("cp", T.inv[:, 0:WIN].indirect(T.offa[:, 0:16]), T.val[:], deps=[t])
+    t = V("ts", T.offa[:], T.fo[:], T.bt[:, 15:16], pqq, A.add, A.add, deps=[t, tw, kpf])
+    t = V("cp", T.inv[:, 0:WIN].indirect(T.offa[:, 0:16]), T.val[:], deps=[t, kval])
     t = V("tt", T.mkd[:], T.inv[:, 0:64], T.mk2[:], A.mult, deps=[t])
     t = V("scan", T.sel[:], T.m4[:], T.mkd[:], 0.0, A.mult, A.add, deps=[t])
     t = V("cp", T.offb[:], T.sel[:, 3:64:4], deps=[t])
     t = V("cp", T.pk[:, 0:256], T.xb[:, 0:1024].indirect(T.offb[:, 0:16]), deps=[t])
-    kpk = V("q", T.oq[:], T.op[:], T.pk[:], deps=[t], key="kpk")
+    kpk = V("q", T.oq[:], T.op[:], T.pk[:], deps=[t, kpz], key="kpk")
 
     c0 = 64 * mine
     oq, pq = T.oq[:, 0:64].bitcast(dt.uint8), T.pq[:, c0:c0 + 64].bitcast(dt.uint8)
     op, pp = T.op[:, 0:64], T.pp[:, c0:c0 + 64]
     wait("g", kpk)
-    loc += write(g, core, list(hcodes), every, oq, T.rq[:].bitcast(dt.uint8), ["rs1"] * len(hcodes), T, topo)
-    loc += write(g, core, list(hplanes), every, op, T.rp[:], ["rs2"] * len(hplanes), T, topo)
-    loc += write(g, core, near, eoff, oq, pq, ["cqA"] * len(near), T, topo)
+    loc += write(g, core, list(road["codes"]), every, oq, T.rq[:].bitcast(dt.uint8), "rs1", T, topo)
+    loc += write(g, core, road["handed"], every, op, T.rp[:], "rs2", T, topo)
+    loc += write(g, core, near, eoff, oq, pq, "cqA", T, topo)
     wait("y", kpk)
     run("y", g.sync.dma_start(pq, oq), "lown", 16)
     run("y", g.sync.dma_start(pp, op), "lown", 16)
 
     t = V("tt", T.m64[:], T.sc[:, 0:64], T.sc[:, 64:128], A.max)
     t = V("tt", T.m32[:], T.m64[:, 0:32], T.m64[:, 32:64], A.max, deps=[t])
-    t = V("tt", T.m16[:], T.m32[:, 0:16], T.m32[:, 16:32], A.max, deps=[t])
-    for i in range(8):
-        t = V("tt", T.eq[:, 16 * i:16 * i + 16], T.sc[:, 16 * i:16 * i + 16], T.m16[:], A.is_equal, deps=[t] if i == 0 else [])
-    t = V("tt", T.eqp[:], T.eq[:], T.prio[:], A.mult, deps=[t])
+    for i in range(2):
+        tm = V("tt", T.m16[:, 16 * i:16 * i + 16], T.m32[:, 0:16], T.m32[:, 16:32], A.max, deps=[t] if i == 0 else [])
+    for i in range(4):
+        t = V("tt", T.eq[:, 32 * i:32 * i + 32], T.sc[:, 32 * i:32 * i + 32], T.m16[:], A.is_equal, deps=[tm] if i == 0 else [])
+    t = V("tt", T.eqp[:], T.eq[:], T.prio[:], A.mult, deps=[t, kpr])
     t = V("tt", T.e64[:], T.eqp[:, 0:64], T.eqp[:, 64:128], A.max, deps=[t])
     t = V("tt", T.e32[:], T.e64[:, 0:32], T.e64[:, 32:64], A.max, deps=[t])
-    t = V("tt", T.pv[:], T.e32[:, 0:16], T.e32[:, 16:32], A.max, deps=[t])
-    for i in range(8):
-        kwin = V("ts", T.win[:, 16 * i:16 * i + 16], T.pv[:], float(8 - rk[i]), None, A.is_equal, deps=[t] if i == 0 else [], key="kwin")
+    for i in range(2):
+        tm = V("tt", T.pv[:, 16 * i:16 * i + 16], T.e32[:, 0:16], T.e32[:, 16:32], A.max, deps=[t] if i == 0 else [])
+    for i in range(4):
+        kwin = V("tt", T.win[:, 32 * i:32 * i + 32], T.pv[:], T.prio[:, 32 * i:32 * i + 32], A.is_equal,
+                 deps=[tm] if i == 0 else [], key="kwin")
     kw2 = S(T.win2[:], T.win[:], deps=[kwin], key="kw2")
+    kwn = S(T.wnv[:], T.pv[:, 0:16], deps=[kwin], key="kwn", scale=-1.0, bias=8.0)
     t = V("scan", T.cum[:], T.rm[:], T.win[:], 0.0, A.mult, A.add, deps=[kwin])
-    kwn = V("ts", T.wnv[:], T.pv[:], -1.0, 8.0, A.mult, A.add, key="kwn")
     t = V("tr", T.t2[:], T.cum[:], deps=[t])
     t = V("scan", T.ts2[:, 1:128], T.t2[:, 0:127], T.rm[:, 1:128], 0.0, A.add, A.mult, deps=[t])
     t = V("tr", T.b2[:], T.ts2[:], deps=[t])
@@ -325,18 +329,25 @@ def rank_program(g, core, T, topo):
     wait("y", kwn)
     run("y", g.sync.dma_start(T.wn[:], T.wnv[:]), "lwn", 16)
 
-    def product(h, half, key, deps):
+    def product(h, half, bank, key, deps):
         wait("t", *deps)
-        return run("t", g.tensor.matmul_mx(T.ps[:, 512 * h:512 * h + 256], T.wq[:, 128 * h:128 * h + 128], T.wp[:, 128 * h:128 * h + 128],
+        return run("t", g.tensor.matmul_mx(T.ps[:, 512 * bank:512 * bank + 256], T.wq[:, 128 * h:128 * h + 128], T.wp[:, 128 * h:128 * h + 128],
                                            T.pq[:, 256 * half:256 * half + 256], T.pp[:, 256 * half:256 * half + 256], True, True), key)
 
-    def drain(h, half, key, k):
+    def drain(h, half, bank, key, k):
         o = 512 * h + 256 * half
-        return S(T.res[:, o:o + 256], T.ps[:, 512 * h:512 * h + 256], deps=[k], key=key)
-    wait("t", ("kwq0", 1), ("kwq1", 1), kpsr, ("lown", 32), ("cqA", sum(arriving(c) for c in near)))
-    da = [drain(h, cls, "da%d" % h, product(h, cls, "ma%d" % h, [])) for h in range(8)]
-    wait("t", ("cqB", sum(arriving(c) for c in far)))
-    db = [drain(h, 1 - cls, "db%d" % h, product(h, 1 - cls, "mb%d" % h, [da[h]])) for h in range(8)]
+        return S(T.res[:, o:o + 256], T.ps[:, 512 * bank:512 * bank + 256], deps=[k], key=key)
+    da, db = {}, {}
+    wait("t", ("kwq0", 1), ("kwq1", 1), kpsr, ("cqB", sum(arriving(c, "codes", "planes") for c in far)))
+    mb = [product(h, 1 - cls, h, "mb%d" % h, []) for h in range(8)]
+    for h in range(FIRST):
+        db[h] = drain(h, 1 - cls, h, "db%d" % h, mb[h])
+    wait("t", ("lown", 32), ("cqA", sum(len(eoff) + arriving(c, "nplanes") for c in near)))
+    for h in range(8):
+        bank = h % FIRST
+        if h >= FIRST:
+            db[h] = drain(h, 1 - cls, h, "db%d" % h, mb[h])
+        da[h] = drain(h, cls, bank, "da%d" % h, product(h, cls, bank, "ma%d" % h, [db[h] if h < FIRST else da[h - FIRST]]))
 
     def found(h, a, b):
         o = 64 * (h // 2 % 2) + 32 * (h // 4) + 16 * (h % 2)

from concourse.bass import DstId, RemoteDMATransfer
from concourse.mybir import dt, AluOpType as A, ActivationFunctionType

N = 8
CODES = "float8_e4m3fn_x4"
ROW = 80
WIN = 17 * ROW
FIRST = 3


def sb(kind, **cols):
    return {k: ("sbuf", [128, n], kind) for k, n in cols.items()}


SCRATCH = {"ps": ("psum", [128, 4096], "float32")}
SCRATCH.update(sb("bfloat16", xb=1024, usl=32, zb=560, pk=512, wz=4096, zz=512))
SCRATCH.update(sb(CODES, zq=140, xq=384, wq=1024, oq=128, pq=512, rq=64))
SCRATCH.update(sb("uint8", zp=140, xp=384, wp=1024, op=128, pp=512, rp=64))
SCRATCH.update(sb("int32", pi=1, pj=4))
SCRATCH.update(sb("float32", pf=4, c64=64, d64=64, m4=64, msk=64, mk2=64, v0=256, val=256, pc0=16, pc=16, qr=1, one=16,
                  rm=128, k8=8, prio=128, rc=8))
SCRATCH.update(sb("float32", rsc=16, sm=64, s32=32, sc=128, repa=64, repb=64, la=64, la2=32, la3=16, pen=16, cb=64, cb2=32,
                  lose=16, tb=32, tt=32, ts=32, bt=32, lp=16, fo=16, inv=WIN, mkd=64, sel=64))
SCRATCH.update(sb("uint16", offa=16, offb=16, off=128))
SCRATCH.update(sb("float32", m64=64, m32=32, m16=32, eq=128, eqp=128, e64=64, e32=32, pv=32, wnv=16, win=128, win2=128, cum=128,
                  t2=128, ts2=128, b2=128, bk=8, cu2=128, pr=128, f64=64, f32=32, x1=32, t1=64, res=4096, ya=256, yb=256))
SEMAPHORES = (["cv", "cw", "loc", "scA", "scB", "cqA", "cqB", "rs0", "rs1", "rs2", "kc",
               "lus", "lx", "lw0", "lw1", "lown", "lwn", "ly",
               "kz", "kzz", "kzs", "kzq", "kxp", "kxq", "ksc", "ksr", "kps", "kpsr", "kio", "kio0", "kpf", "kpz", "kval",
               "kpr", "kw0", "kw1", "kwq0", "kwq1",
               "kpk", "kwn", "kwin", "kw2", "ky0", "ky1"] + ["%s%d" % (k, h) for k in ("ma", "da", "mb", "db") for h in range(8)])


def order(T, topo):
    a = [c for c in T.cores if c == T.cores[0] or topo.may_write(T.cores[0], c)]
    return [a, [c for c in T.cores if c not in a]]


def roads(core, T, topo):
    two = order(T, topo)
    own, far = two if core in two[0] else two[::-1]
    near = [c for c in own if c != core]
    cand = [c for c in topo.cores_of(core) if c not in T.cores and all(topo.may_write(c, d) for d in far)]
    a = [c for c in cand if topo.die(c) != topo.die(core)]
    b = [c for c in cand if topo.die(c) == topo.die(core)]
    hc, hp = [a[0], b[0]], [a[1], b[1]]
    k = own.index(core)
    codes = {h: [d for j, d in enumerate(far) if (j + k) % 2 == i] for i, h in enumerate(hc)}
    planes = {h: [d for j, d in enumerate(far) if (j + k) % 2 == i] for i, h in enumerate(hp)}
    nplanes = dict(zip(hc + [hp[k % 2]], [[d] for d in near]))
    scores = {h: [d for j, d in enumerate(far) if (j + k) % 4 == i] for i, h in enumerate(hc + hp)}
    return {"near": near, "far": far, "codes": codes, "planes": planes, "nplanes": nplanes, "scores": scores,
            "handed": hp + [h for h in hc if h in nplanes]}


def bits(engines):
    return sum(1 << e for e in engines)


def write(g, core, dests, engines, src, dst, sem, T, topo):
    i = []
    for d in dests:
        rid, pid = topo.addr(d, core)
        i.append(DstId(rid=rid, pnc=pid))
    g.remote_dma_fused([RemoteDMATransfer(dst_ids=i, dma_engine_mask=bits(engines), remote_sem=T.sem[sem],
                                          srcs=[src], dsts=[dst] * len(i))], local_sem=T.sem.loc)
    return len(engines)


def engines_of(core, near, helper, topo):
    off, every = topo.engines(core, near), topo.engines(core, helper)
    return off, [e for e in every if e not in off], every


def relay(g, core, boss, T, topo):
    r = roads(boss, T, topo)
    if core not in r["scores"]:
        return
    p = sum(order(T, topo), []).index(boss)
    eng = topo.engines(core, r["far"][0])
    _, eon, every = engines_of(boss, r["near"][0], core, topo)
    half, what = list(r["scores"]).index(core) % 2, list(r["scores"]).index(core) // 2
    step, base, buf = ((0, 1, T.one), (1, 8 * half, T.pc0))[what]
    g.iota(T.rc[:], [[step, 8]], base, 0, allow_small_or_imprecise_dtypes=True).then_inc(T.sem.kio, 1)
    g.wait_ge(T.sem.kio, 1)
    n = write(g, core, [boss], eng, T.rc[:], buf[:, 8 * half:8 * half + 8], "kc", T, topo)
    g.wait_ge(T.sem.rs0, len(eon))
    n += write(g, core, r["scores"][core], eng, T.rsc[:], T.sc[:, 16 * p:16 * p + 16], "scB", T, topo)
    if core in r["codes"]:
        g.wait_ge(T.sem.rs1, len(every))
        n += write(g, core, r["codes"][core], eng, T.rq[:].bitcast(dt.uint8), T.pq[:, 64 * p:64 * p + 64].bitcast(dt.uint8),
                   "cqB", T, topo)
    if core in r["handed"]:
        g.wait_ge(T.sem.rs2, len(every))
    for road, sem in (("planes", "cqB"), ("nplanes", "cqA")):
        if core in r[road]:
            n += write(g, core, r[road][core], eng, T.rp[:], T.pp[:, 64 * p:64 * p + 64], sem, T, topo)
    g.wait_ge(T.sem.loc, n)


def rank_program(g, core, T, topo):
    rank = T.rank_of(core)
    if rank is None:
        for boss in T.cores:
            if core in topo.cores_of(boss):
                relay(g, core, boss, T, topo)
        return
    road = roads(core, T, topo)
    near, far = road["near"], road["far"]
    two = order(T, topo)
    pieces = two[0] + two[1]
    cls = 0 if core in two[0] else 1
    mine = pieces.index(core)
    idx = two[cls].index(core)
    rk = [T.rank_of(c) for c in pieces]

    Q = {"v": [g.vector, "cv"], "s": [g.scalar, None], "t": [g.tensor, None], "g": [g, None], "y": [g.sync, None]}
    total = {}
    seen = {q: {} for q in Q}

    def wait(q, *deps):
        for d in deps:
            if d is None:
                continue
            sem, val = d
            if sem in ("cv", "cw"):
                val = total[sem]
            if seen[q].get(sem, 0) < val:
                Q[q][0].wait_ge(T.sem[sem], val)
                seen[q][sem] = val

    def run(q, ins, key=None, n=1):
        sem = key or Q[q][1]
        ins.then_inc(T.sem[sem], n)
        total[sem] = total.get(sem, 0) + n
        return (sem, total[sem])

    def V(name, *args, deps=(), key=None):
        wait("v", *deps)
        f = {"set": g.vector.memset, "cp": g.vector.tensor_copy, "tt": g.vector.tensor_tensor, "ts": g.vector.tensor_scalar,
             "scan": g.vector.tensor_tensor_scan, "tr": g.vector.transpose, "q": g.vector.quantize_mx}[name]
        return run("v", f(*args), key)

    def S(out, in_, deps=(), key=None, **line):
        wait("s", *deps)
        return run("s", g.scalar.activation(out, in_, ActivationFunctionType.Identity if line else ActivationFunctionType.Copy, **line), key)

    def iota(out, pattern, base, cm, key="kio"):
        return run("g", g.iota(out, pattern, base, cm, allow_small_or_imprecise_dtypes=True), key)

    lus = run("y", g.sync.dma_start(T.usl[:], T.us[:, 0:32]), "lus", 16)
    lx = run("s", g.scalar.dma_start(T.xb[:], T.x[:]), "lx", 16)

    iota(T.pi[:], [[0, 1]], 0, 1, "kio0")
    kio0 = iota(T.c64[:], [[1, 4], [0, 16]], 0, 0, "kio0")
    iota(T.d64[:], [[0, 16], [1, 4]], 0, 0)
    iota(T.k8[:], [[64, 8]], -1, 0)
    kio = iota(T.v0[:], [[4, 16], [64, 16]], 0, 0)

    kzz = V("set", T.zz[:], 0.0, key="kzz")
    kz = V("set", T.zb[:], 0.0, key="kz")
    kxp = V("q", T.xq[:, 256:384], T.xp[:, 256:384], T.zz[:], deps=[kzz], key="kxp")

    def zero(block, key):
        return S(T.wz[:, 512 * block:512 * block + 512], T.zz[:], deps=[kzz], key=key)
    zero(0, "kw0")
    zero(1, "kw0")
    zs = ksz = None
    for l in range(4):
        for e in range(4):
            a = 4 * (12 + l) + e
            o, i = T.zb[:, a:a + 449:64], T.usl[:, e:32:4]
            if l < 2:
                zs = V("cp", o, i, deps=[kz, lus])
            else:
                ksz = S(o, i, deps=[kz, lus], key="kzs")
    kzq = V("q", T.zq[:], T.zp[:], T.zb[:], deps=[zs, ksz], key="kzq")
    kxq = V("q", T.xq[:, 0:256], T.xp[:, 0:256], T.xb[:], deps=[lx], key="kxq")
    zero(2, "kw0")
    kw0 = zero(3, "kw0")
    zero(4, "kw1")
    zero(5, "kw1")
    wait("v", kio0)
    V("ts", T.pj[:, 0:1], T.pi[:], 3, None, A.bitwise_and)
    V("ts", T.pj[:, 1:2], T.pi[:], 2, 3, A.arith_shift_right, A.bitwise_and)
    t = V("ts", T.pj[:, 2:3], T.pi[:], 15, None, A.bitwise_and)
    kpf = V("cp", T.pf[:, 0:3], T.pj[:, 0:3], deps=[t], key="kpf")
    pt, pa, pqq = T.pf[:, 0:1], T.pf[:, 1:2], T.pf[:, 2:3]
    tm = V("ts", T.msk[:], T.c64[:], pt, None, A.is_equal, deps=[kpf])

    wait("t", kzq, kxp, kxq)
    for i in range(4):
        m = g.tensor.matmul_mx(T.ps[:, 0:128], T.zq[:, 12 - 4 * i:140 - 4 * i], T.zp[:, 12 - 4 * i:140 - 4 * i],
                               T.xq[:, 64 * i:64 * i + 128], T.xp[:, 64 * i:64 * i + 128], i == 0, i == 3)
    kps = run("t", m, "kps")
    kpsr = V("tt", T.sm[:], T.ps[:, 0:64], T.msk[:], A.mult, deps=[kps, tm], key="kpsr")
    t = V("tt", T.s32[:], T.sm[:, 0:32], T.sm[:, 32:64], A.add, deps=[kpsr])
    own = T.sc[:, 16 * mine:16 * mine + 16]
    ksc = V("tt", own, T.s32[:, 0:16], T.s32[:, 16:32], A.add, deps=[t], key="ksc")

    hs = list(road["scores"])
    eoff, eon, every = engines_of(core, near[0], hs[0], topo)
    nA = len(near) * len(eoff)
    theirs = {c: roads(c, T, topo) for c in near + far}

    def arriving(c, *kinds):
        return sum(len(topo.engines(h, core)) for k in kinds for h, d in theirs[c][k].items() if core in d)
    nB = sum(arriving(c, "scores") for c in far)
    kc = ("kc", sum(len(topo.engines(h, far[0])) for h in hs))
    wait("g", ksc)
    loc = write(g, core, hs, eon, own, T.rsc[:], "rs0", T, topo)
    loc += write(g, core, near, eoff, own, own, "scA", T, topo)

    ksr = None
    for i in range(4):
        ksr = S(T.repa[:, 16 * i:16 * i + 16], own, deps=[ksc], key="ksr")
    kpz = S(T.pk[:, 256:512], T.zz[:, 0:256], deps=[kzz], key="kpz")
    zero(6, "kw1")
    kw1 = zero(7, "kw1")
    t = V("set", T.rm[:], 1.0)
    V("set", T.la[:, 16 * idx:16 * idx + 16], 0.0)
    V("set", T.tb[:], 0.0)
    V("set", T.ts[:], 0.0)
    V("set", T.ts2[:, 0:1], 0.0)
    V("set", T.inv[:, 0:64], 0.0)
    V("set", T.rm[:, 0:128:16], 0.0, deps=[t])
    kval = S(T.val[:], T.v0[:], deps=[kio, kpf], key="kval", bias=pt)
    for i in range(8):
        kpr = S(T.prio[:, 16 * i:16 * i + 16], T.one[:], deps=[kc], key="kpr", scale=float(8 - rk[i]))
    for half, kw in enumerate((kw0, kw1)):
        wait("y", kw)
        for h in range(4 * half, 4 * half + 4):
            run("y", g.sync.dma_start(T.wz[16 * h:16 * h + 16, 512 * h:512 * h + 512], T.w[16 * h:16 * h + 16, :]), "lw%d" % half, 16)

    def wquant(half):
        V("q", T.wq[:, 512 * half:512 * half + 512], T.wp[:, 512 * half:512 * half + 512],
          T.wz[:, 2048 * half:2048 * half + 2048], deps=[("lw%d" % half, 64)], key="kwq%d" % half)
    wait("v", kio)
    V("ts", T.m4[:], T.d64[:], 1.0, None, A.min)
    V("ts", T.mk2[:], T.d64[:], pa, None, A.is_equal)
    t = V("ts", T.qr[:], pqq, float(ROW), float(ROW + 1), A.mult, A.add)
    wquant(0)
    V("ts", T.pc[:], T.pc0[:], T.qr[:], None, A.add, deps=[t, kc])

    ca, cb = 64 * cls, 64 * (1 - cls)
    wait("v", ksr, ("scA", nA), ksc)
    a = 16 * idx
    if idx > 0:
        t = V("tt", T.la[:, 0:a], T.sc[:, ca:ca + a], T.repa[:, 0:a], A.is_ge)
    if idx < 3:
        t = V("tt", T.la[:, a + 16:64], T.sc[:, ca + a + 16:ca + 64], T.repa[:, a + 16:64], A.is_gt)
    t = V("tt", T.la2[:], T.la[:, 0:32], T.la[:, 32:64], A.max, deps=[t])
    t = V("tt", T.la3[:], T.la2[:, 0:16], T.la2[:, 16:32], A.max, deps=[t])
    t = V("ts", T.pen[:], T.la3[:], -1e28, None, A.mult, deps=[t])
    for i in range(4):
        tr = V("tt", T.repb[:, 16 * i:16 * i + 16], own, T.pen[:], A.add, deps=[t] if i == 0 else [])
    wquant(1)

    wait("v", tr, ("scB", nB))
    low = 16 * len([c for c in far if T.rank_of(c) < rank])
    if low > 0:
        t = V("tt", T.cb[:, 0:low], T.sc[:, cb:cb + low], T.repb[:, 0:low], A.is_ge)
    if low < 64:
        t = V("tt", T.cb[:, low:64], T.sc[:, cb + low:cb + 64], T.repb[:, low:64], A.is_gt)
    t = V("tt", T.cb2[:], T.cb[:, 0:32], T.cb[:, 32:64], A.max, deps=[t])
    t = V("tt", T.lose[:], T.cb2[:, 0:16], T.cb2[:, 16:32], A.max, deps=[t])
    t = V("scan", T.tb[:, 0:16], T.one[:], T.lose[:], -1.0, A.add, A.subtract, deps=[t, kc])
    tw = V("tt", T.lp[:], T.lose[:], T.pc[:], A.mult, key="cw")
    t = V("tr", T.tt[:], T.tb[:], deps=[t])
    tw = V("tt", T.fo[:], T.tb[:, 0:16], T.lp[:], A.add, deps=[tw], key="cw")
    t = V("scan", T.ts[:, 1:32], T.tt[:, 0:31], T.rm[:, 1:32], 0.0, A.add, A.mult, deps=[t])
    t = V("tr", T.bt[:], T.ts[:], deps=[t])
    t = V("ts", T.offa[:], T.fo[:], T.bt[:, 15:16], pqq, A.add, A.add, deps=[t, tw, kpf])
    t = V("cp", T.inv[:, 0:WIN].indirect(T.offa[:, 0:16]), T.val[:], deps=[t, kval])
    t = V("tt", T.mkd[:], T.inv[:, 0:64], T.mk2[:], A.mult, deps=[t])
    t = V("scan", T.sel[:], T.m4[:], T.mkd[:], 0.0, A.mult, A.add, deps=[t])
    t = V("cp", T.offb[:], T.sel[:, 3:64:4], deps=[t])
    t = V("cp", T.pk[:, 0:256], T.xb[:, 0:1024].indirect(T.offb[:, 0:16]), deps=[t])
    kpk = V("q", T.oq[:], T.op[:], T.pk[:], deps=[t, kpz], key="kpk")

    c0 = 64 * mine
    oq, pq = T.oq[:, 0:64].bitcast(dt.uint8), T.pq[:, c0:c0 + 64].bitcast(dt.uint8)
    op, pp = T.op[:, 0:64], T.pp[:, c0:c0 + 64]
    wait("g", kpk)
    loc += write(g, core, list(road["codes"]), every, oq, T.rq[:].bitcast(dt.uint8), "rs1", T, topo)
    loc += write(g, core, road["handed"], every, op, T.rp[:], "rs2", T, topo)
    loc += write(g, core, near, eoff, oq, pq, "cqA", T, topo)
    wait("y", kpk)
    run("y", g.sync.dma_start(pq, oq), "lown", 16)
    run("y", g.sync.dma_start(pp, op), "lown", 16)

    t = V("tt", T.m64[:], T.sc[:, 0:64], T.sc[:, 64:128], A.max)
    t = V("tt", T.m32[:], T.m64[:, 0:32], T.m64[:, 32:64], A.max, deps=[t])
    for i in range(2):
        tm = V("tt", T.m16[:, 16 * i:16 * i + 16], T.m32[:, 0:16], T.m32[:, 16:32], A.max, deps=[t] if i == 0 else [])
    for i in range(4):
        t = V("tt", T.eq[:, 32 * i:32 * i + 32], T.sc[:, 32 * i:32 * i + 32], T.m16[:], A.is_equal, deps=[tm] if i == 0 else [])
    t = V("tt", T.eqp[:], T.eq[:], T.prio[:], A.mult, deps=[t, kpr])
    t = V("tt", T.e64[:], T.eqp[:, 0:64], T.eqp[:, 64:128], A.max, deps=[t])
    t = V("tt", T.e32[:], T.e64[:, 0:32], T.e64[:, 32:64], A.max, deps=[t])
    for i in range(2):
        tm = V("tt", T.pv[:, 16 * i:16 * i + 16], T.e32[:, 0:16], T.e32[:, 16:32], A.max, deps=[t] if i == 0 else [])
    for i in range(4):
        kwin = V("tt", T.win[:, 32 * i:32 * i + 32], T.pv[:], T.prio[:, 32 * i:32 * i + 32], A.is_equal,
                 deps=[tm] if i == 0 else [], key="kwin")
    kw2 = S(T.win2[:], T.win[:], deps=[kwin], key="kw2")
    kwn = S(T.wnv[:], T.pv[:, 0:16], deps=[kwin], key="kwn", scale=-1.0, bias=8.0)
    t = V("scan", T.cum[:], T.rm[:], T.win[:], 0.0, A.mult, A.add, deps=[kwin])
    t = V("tr", T.t2[:], T.cum[:], deps=[t])
    t = V("scan", T.ts2[:, 1:128], T.t2[:, 0:127], T.rm[:, 1:128], 0.0, A.add, A.mult, deps=[t])
    t = V("tr", T.b2[:], T.ts2[:], deps=[t])
    t = V("tt", T.bk[:], T.b2[:, 15:128:16], T.k8[:], A.add, deps=[t])
    t = V("tt", T.win2[:, 0:128:16], T.win2[:, 0:128:16], T.bk[:], A.add, deps=[t, kw2])
    t = V("scan", T.cu2[:], T.rm[:], T.win2[:], 0.0, A.mult, A.add, deps=[t])
    t = V("tt", T.pr[:], T.cu2[:], T.win[:], A.mult, deps=[t])
    t = V("tt", T.f64[:], T.pr[:, 0:64], T.pr[:, 64:128], A.add, deps=[t])
    t = V("tt", T.f32[:], T.f64[:, 0:32], T.f64[:, 32:64], A.add, deps=[t])
    V("tt", T.x1[:, 0:16], T.f32[:, 0:16], T.f32[:, 16:32], A.add, deps=[t])
    t = V("tt", T.x1[:, 16:32], T.f32[:, 0:16], T.f32[:, 16:32], A.add)
    V("tr", T.t1[0:64, 0:32], T.x1[0:64, :], deps=[t])
    t = V("tr", T.t1[64:128, 32:64], T.x1[64:128, :])
    V("cp", T.t1[64:128, 0:32], T.t1[0:64, 0:32], deps=[t])
    t = V("cp", T.t1[0:64, 32:64], T.t1[64:128, 32:64])
    for e in range(2):
        for b in range(4):
            a = b // 2 * 2 + e
            t = V("cp", T.off[32 * b:32 * b + 32, 64 * e:64 * e + 64], T.t1[32 * a:32 * a + 32, 0:64], deps=[t] if e + b == 0 else [])
    toff = t
    wait("y", kwn)
    run("y", g.sync.dma_start(T.wn[:], T.wnv[:]), "lwn", 16)

    def product(h, half, bank, key, deps):
        wait("t", *deps)
        return run("t", g.tensor.matmul_mx(T.ps[:, 512 * bank:512 * bank + 256], T.wq[:, 128 * h:128 * h + 128], T.wp[:, 128 * h:128 * h + 128],
                                           T.pq[:, 256 * half:256 * half + 256], T.pp[:, 256 * half:256 * half + 256], True, True), key)

    def drain(h, half, bank, key, k):
        o = 512 * h + 256 * half
        return S(T.res[:, o:o + 256], T.ps[:, 512 * bank:512 * bank + 256], deps=[k], key=key)
    da, db = {}, {}
    wait("t", ("kwq0", 1), ("kwq1", 1), kpsr, ("cqB", sum(arriving(c, "codes", "planes") for c in far)))
    mb = [product(h, 1 - cls, h, "mb%d" % h, []) for h in range(8)]
    for h in range(FIRST):
        db[h] = drain(h, 1 - cls, h, "db%d" % h, mb[h])
    wait("t", ("lown", 32), ("cqA", sum(len(eoff) + arriving(c, "nplanes") for c in near)))
    for h in range(8):
        bank = h % FIRST
        if h >= FIRST:
            db[h] = drain(h, 1 - cls, h, "db%d" % h, mb[h])
        da[h] = drain(h, cls, bank, "da%d" % h, product(h, cls, bank, "ma%d" % h, [db[h] if h < FIRST else da[h - FIRST]]))

    def found(h, a, b):
        o = 64 * (h // 2 % 2) + 32 * (h // 4) + 16 * (h % 2)
        return T.res[:, 512 * h:512 * h + 512].indirect(T.off[:, o + a // 16:o + b // 16])
    out, prev = T.ya, T.yb
    acc = V("cp", out[:], found(0, 0, 256), deps=[toff, da[0], db[0]])
    for h in range(1, 7):
        out, prev = prev, out
        acc = V("tt", out[:], found(h, 0, 256), prev[:], A.add, deps=[acc, da[h], db[h]])
    out, prev = prev, out
    for i, q in enumerate(("y", "s")):
        a, b = 128 * i, 128 * i + 128
        k = V("tt", out[:, a:b], found(7, a, b), prev[:, a:b], A.add, deps=[acc, da[7], db[7]], key="ky%d" % i)
        wait(q, k)
        run(q, Q[q][0].dma_start(T.y[:, a:b], out[:, a:b]), "ly", 16)

    wait("g", ("ly", 32), ("lwn", 16), ("loc", loc))
    g.wait_ge(T.sem.cv, total["cv"])
